import numpy as np, ml_dtypes
CORES = [16,18,20,22]
N = 4
BF = ml_dtypes.bfloat16
S, R, NF, PH, LB, RO = 4096, 4096, 256, 512, 9, 5
def place(s, p):
    return ((s * p >> 4) + s + 37 * p) & (R - 1)
def records(rng):
    st = ((np.arange(8)[None, :] + rng.integers(0, 3, (N, 1))) % 3)[:, :, None, None]
    lo = np.where(st == 0, 0, np.where(st == 1, 64 * rng.integers(0, 4, (N, 8, 1, R)), 200 * (rng.random((N, 8, 1, R)) < 0.35))).astype(np.int32)
    span = np.where(st == 0, 256, np.where(st == 1, 64, 56)).astype(np.float32)
    x = np.minimum(lo + (rng.random((N, 8, 16, R), dtype=np.float32) * span).astype(np.int32), 255)
    u = rng.random((N, 8, 16, 1))
    th = np.where(st == 0, 1000 + 700 * u, np.where(st == 1, 256 + 2000 * u, 450 + 1150 * u)).astype(np.int64)
    return x, th
def parts(rng):
    var = rng.choice(np.array([0.2, 0.35, 0.5]), (N, 8, 1, 1)); emp = rng.choice(np.array([0.2, 0.45, 0.7]), (N, 8, 1, 1))
    tk = rng.integers(0, S, (N, 8, 16, S)) + S * (rng.random((N, 8, 16, S)) < var)
    fr = np.where(rng.random((N, 8, 16, NF)) < emp, -1, rng.integers(0, S * PH, (N, 8, 16, NF)))
    return tk, fr, rng.integers(0, S, (N, 8, NF)), rng.integers(0, NF, (N, 8, NF)), rng.integers(0, S, (N, 8, NF))
def pack(x, tk, fr, th, s, f, c):
    return {"x": np.ascontiguousarray(x.reshape(N, 128, R)).astype(np.float32).astype(BF), "sk": np.ascontiguousarray(tk.reshape(N, 128, S)).astype(np.int32),
            "fr": np.ascontiguousarray(fr.reshape(N, 128, NF)).astype(np.int32), "th": np.ascontiguousarray(th.reshape(N, 128, 1)).astype(np.int32),
            "gs": s.astype(np.int32), "gf": f.astype(np.int32), "gcl": c.astype(np.int32)}
def setup_inputs(rng):
    x, th = records(rng); tk, fr, s, f, c = parts(rng)
    return pack(x, tk, fr, th, s, f, c)
def setup_inputs_spread(rng):
    amp = np.exp2(8 * rng.random((N, 8, 1, R))).astype(np.float32)
    x = np.minimum((rng.random((N, 8, 16, R), dtype=np.float32) * amp).astype(np.int32), 255)
    x = np.where(rng.random((N, 8, 1, R)) < 0.0625, 255 - x, x)
    th = np.minimum(np.exp2(12 * rng.random((N, 8, 16, 1))).astype(np.int64), 4080)
    u = rng.random((N, 8, 16, S)); tk = np.minimum((2 * S * u * np.sqrt(u)).astype(np.int64), 2 * S - 1)
    v = rng.random((N, 8, 16, NF)); fr = np.where(rng.random(v.shape) < 0.3 * rng.random((N, 8, 1, 1)) + 0.1, -1, np.minimum((S * PH * v * v).astype(np.int64), S * PH - 1))
    w = rng.random((3, N, 8, NF)); w = w * w
    return pack(x, tk, fr, th, np.minimum((S * w[0]).astype(np.int64), S - 1), np.minimum((NF * w[1]).astype(np.int64), NF - 1), np.minimum((S * w[2]).astype(np.int64), S - 1))
def setup_inputs_ends(rng):
    one = rng.random((N, 8, 1, R)) < 0.5; each = rng.random((N, 8, 16, R)) < 0.5
    x = 255 * np.where(rng.random((N, 8, 1, R)) < 0.25, each, one).astype(np.int64)
    tk = (2 * S - 1) * rng.integers(0, 2, (N, 8, 16, S)); fr = np.where(rng.integers(0, 2, (N, 8, 16, NF)) == 1, S * PH - 1, -1)
    s = (S - 1) * rng.integers(0, 2, (N, 8, NF)); f = (NF - 1) * rng.integers(0, 2, (N, 8, NF)); c = (S - 1) * rng.integers(0, 2, (N, 8, NF))
    th = np.full((N, 8, 16, 1), 4080, np.int64)
    for a in range(N):
        for g in range(8):
            if g == 7: z = rng.permutation(15)[:9 if a % 2 == 0 else 7]
            else: z = rng.permutation(16)[:16 if g == 6 else 8]
            th[a, g, z, 0] = 0
    s[:, :, NF - 1] = S - 1; f[:, :, NF - 1] = NF - 1; c[:, :, NF - 1] = 0
    tk[::2, :, :, S - 1] = 2 * S - 1; tk[::2, :, :, 0] = 0; tk[:, 7, :, S - 1] = 2 * S - 1; tk[:, 7, :, 0] = 0
    x[..., place(S - 1, PH - 1)] = 255; x[..., place(S - 1, NF - 1)] = 255; x[..., place(0, NF - 1)] = 0
    return pack(x, tk, fr, th, s, f, c)
def setup_inputs_corners(rng):
    x, th = records(rng); tk, fr, s, f, c = parts(rng); i = np.arange(NF); even = i % 2 == 0
    near = np.array([[3, 21], [21, 3], [5, 19], [19, 5], [7, 9], [9, 7]])
    for a in range(N):
        o = rng.permutation(8)
        tk[a, o[0]] = tk[a, o[0]] & (S - 1); fr[a, o[0]] = -1
        tk[a, o[1]] = (tk[a, o[1]] & (S - 1)) + S; fr[a, o[1]] = -1
        tk[a, o[2]] = (tk[a, o[2]] & (S - 1)) + S
        fr[a, o[2]] = PH * rng.integers(0, S, (16, NF)) + np.where(rng.random((16, NF)) < 0.5, i, NF + i)
        f[a, o[3]] = i; fr[a, o[3]] = np.where(i % 2 == 0, -1, rng.integers(0, S * PH, (16, NF)))
        f[a, o[4]] = rng.choice(np.array([0, NF - 1]), NF); s[a, o[4]] = rng.choice(np.array([0, S - 1]), NF); c[a, o[4]] = np.where(rng.random(NF) < 0.5, s[a, o[4]], S - 1 - s[a, o[4]])
        fr[a, o[4]] = np.where(rng.random((16, NF)) < 0.4, -1, PH * rng.choice(np.array([0, S - 1]), (16, NF)) + rng.choice(np.array([0, NF - 1, NF, PH - 1]), (16, NF)))
        th[a, o[5]] = 4080; th[a, o[6]] = 0; th[a, o[7]] = 4080; th[a, o[7], rng.permutation(16)[:8]] = 0
        f[a, o[5]] = np.where(even, i, f[a, o[5]]); c[a, o[5]] = np.where(even, s[a, o[5]], c[a, o[5]]); fr[a, o[5]] = np.where(even, -1, fr[a, o[5]])
        pq = near[rng.integers(0, 6, NF)]
        s[a, o[6]] = np.where(even, S - pq[:, 0], s[a, o[6]]); c[a, o[6]] = np.where(even, S - pq[:, 1], c[a, o[6]])
    return pack(x, tk, fr, th, s, f, c)
def setup_inputs_ties(rng):
    v, th = records(rng); tk, fr, s, f, c = parts(rng)
    x = np.broadcast_to(60 * rng.integers(0, 5, (N, 8, 1, R)), (N, 8, 16, R)).copy()
    th = rng.choice(np.array([959, 960, 961, 1919, 1920, 1921]), (N, 8, 16, 1))
    off = rng.integers(0, 4, (N, 2, 16, R)) * (rng.random((N, 2, 1, R)) < 0.5)
    x[:, 1::4] = np.abs(255 * rng.integers(0, 2, (N, 2, 1, R)) - off)
    lev = np.array([0, 0, 0, 24, 24, 24, 4048, 4056, 4060, 4064, 4078, 4079, 4079, 4079, 4080, 4080])
    th[:, 1::4] = lev[np.argsort(rng.random((N, 2, 16, 1)), axis=2)]
    few = rng.integers(0, S, (N, 4, 3)); which = rng.integers(0, 3, (2, N, 4, NF))
    s[:, ::2] = np.take_along_axis(few, which[0], 2); c[:, ::2] = np.take_along_axis(few, which[1], 2); f[:, ::2] = rng.integers(0, 4, (N, 4, NF))
    return pack(x, tk, fr, th, s, f, c)
def check_inputs(d):
    bad = []
    for k, lo, hi in (("x", 0, 255), ("sk", 0, 2 * S - 1), ("fr", -1, S * PH - 1), ("th", 0, 4080), ("gs", 0, S - 1), ("gf", 0, NF - 1), ("gcl", 0, S - 1)):
        if k not in d: bad.append("no " + k); continue
        v = np.asarray(d[k]).astype(np.float64)
        if not (np.min(v) >= lo and np.max(v) <= hi): bad.append("range of " + k)
        elif np.any(v != np.floor(v)): bad.append("whole numbers in " + k)
    return bad
def reference(x, sk, fr, th, gs, gf, gcl):
    X = x.astype(np.float32).astype(np.int32).reshape(N, 8, 16, R); T = sk.astype(np.int64).reshape(N, 8, 16, S); lim = th.astype(np.int64).reshape(N, 8, 16, 1)
    own = fr.astype(np.int64).reshape(N, 8, 16, NF); F = np.concatenate([own, own], axis=3)
    i = np.arange(NF); mark = np.zeros((N, 8, 16, NF), bool); A = np.zeros((N, NF), np.int64)
    s = gs.astype(np.int64); f = gf.astype(np.int64); c = gcl.astype(np.int64); h = np.zeros_like(s) + i
    s0 = s; f0 = f; c0 = c
    def molecules(a, b):
        v = np.take_along_axis(T, a[:, :, None, :], 3); w = np.take_along_axis(F, b[:, :, None, :], 3)
        return np.where((v >= S) & (w >= 0), w, (v & (S - 1)) * PH + b[:, :, None, :]), (v >= S) & (w < 0)
    def pick(m):
        return np.take_along_axis(X, place(m >> LB, m & (PH - 1)).reshape(N, 8, 1, 16 * NF), 3)
    for rnd in range(RO):
        goal, _ = molecules(s, f); clause, hole = molecules(c, h)
        free = hole & (h == i)[:, :, None, :]; clause = np.where(free, goal, clause)
        D = np.add.reduce(np.abs(pick(goal) - pick(clause)), axis=2).astype(np.int64).reshape(N, 8, 16, NF)
        over = D > lim; clash = np.add.reduce(over.astype(np.int64), axis=2) >= 8 + (A & 1)[:, None, :]
        m = np.argmax(np.where(over, -1, D), axis=2)[:, :, None, :]
        gm = np.take_along_axis(goal, m, 2)[:, :, 0]; cm = np.take_along_axis(clause, m, 2)[:, :, 0]
        dm = np.take_along_axis(D, m, 2)[:, :, 0]; tm = np.take_along_axis(np.broadcast_to(lim, D.shape), m, 2)[:, :, 0]
        save = ~clash & (2 * dm < tm)
        bind = free & ~clash[:, :, None, :]
        own = np.where(mark & clash[:, :, None, :], -1, np.where(bind, goal, own))
        mark = (mark | bind) & ~(clash | save)[:, :, None, :]
        nxt = ((c0 * s0 >> 5) + c0 + 1) & (S - 1)
        s = np.where(clash, s0, gm >> LB); f = np.where(clash, f0, gm & (PH - 1))
        c = np.where(clash, nxt, cm >> LB); h = np.where(clash, i, cm & (PH - 1))
        s0 = np.where(save, s, s0); f0 = np.where(save, f, f0); c0 = np.where(clash, nxt, np.where(save, c, c0))
        A = np.add.reduce(clash.astype(np.int64), axis=1)
        F = np.concatenate([own, F[..., NF:]], axis=3)
        if rnd < RO - 1:
            d = 1 + rnd % (N - 1); col = np.take_along_axis(F, f[:, :, None, :], 3)
            F = np.concatenate([own, np.roll(col, d, axis=0)], axis=3); s = np.roll(s, d, axis=0); f = np.zeros_like(s) + NF + i
    return {"yf": np.where(own < 0, -1, 2 * own + mark).reshape(N, 128, NF).astype(np.float32), "yg": (PH * s + f).astype(np.float32), "yc": (PH * c + h).astype(np.float32),
            "ysg": (PH * s0 + f0).astype(np.float32), "yk": c0.astype(np.float32)}

@@ -1,0 +1,497 @@
+from concourse.mybir import AluOpType, ActivationFunctionType
+
+OP = AluOpType
+AF = ActivationFunctionType
+U = 1 << 22
+NF, RO, N = 256, 5, 4
+H = (0, 1)
+F32, BF, I32, U16 = "float32", "bfloat16", "int32", "uint16"
+SCRATCH = {}
+
+
+def _bufs(where, dtype, text):
+    for w in text.split():
+        n, c = w.split(":")
+        r, c = (c.split("x") if "x" in c else (128, c))
+        SCRATCH[n] = (where, [int(r), int(c)], dtype)
+
+
+_bufs("sbuf", F32, "skv:4096 skt:4096 inf:8x512 ine:8x512 thf:8 tabb:768 tabh:768 j8:8 mske:256 rst:256 idf:128 onef:128 thrt:256 "
+      "iw:16 il:16 eight:16 lim:16 fb:256 hb:256 hi:256 tg:256 tc:256 f3p:256 own3:256 x3:256 eqm:256 nov:256 key:256 cnt:256 sm:256 "
+      "cl:16 smx:16 pgc:512 thp:256 st:16 clst:32 lsb:32 lh:512 we:16 wf:16 wh:16 sc:32 ns:16 sv:32 s1:32 s2:32 t1:16 "
+      "fot:64x128 oy:256 oy2:256 oz:256 f0:768 f1:768 f2:768 f3:768 f4:768 snd0:256 snd1:256 snd2:256 snd3:256")
+_bufs("sbuf", BF, "idk:128 xr:4096 ub:4096 wb:4096 df:4096 ab:4096 b16:8 idb:128 nidb:128 k0:8 rcb:256 oneb:128 krow:128 fr5:256 mk2:256 sel:256 lhb:512")
+_bufs("sbuf", I32, "ski:4096 ini:8x768 fri:256 thi:8 thj:8 pi:256 ci:256 pm:256 cm:256 ps:8 rawg:256 rawc:256 ga:256 ca:256 "
+      "pg:256 qg:256 prg:256 rg:256 pc:256 qc:256 prc:256 rc:256 wi:32 wq:32 pai:16 paj:16 s3:32 t4:16 t5:16 t6:16 t7:16 t8:16 fip:64 oi:256 op:256")
+_bufs("sbuf", U16, "ug:256 uc:256 el:16 fl:16 hl:16 sl:160 sarr:80")
+_bufs("psum", F32, "b0:512 b1:512 pe:512 pl:512 pr:512 sr:512 d0:512 d1:512")
+SEMAPHORES = ["sv", "ss", "st", "sg", "rl"] + ["as%d" % t for t in range(4)] + ["ac%d" % t for t in range(4)] + ["d%d" % t for t in range(24)]
+VIEW = {"sks": ("df", 0, 4096), "frs": ("op", 0, 256), "frm": ("oy", 0, 256), "dg": ("oz", 0, 128), "fin": ("lh", 0, 64), "fiq": ("lh", 64, 64), "fim": ("lh", 128, 64)}
+PSUM = [n for n in SCRATCH if SCRATCH[n][0] == "psum"]
+GCH = [(0, 1024), (1024, 2048), (2048, 3072), (3072, 4096)]
+VCH = [(0, 1024), (1024, 2048), (2048, 3072), (3072, 3584), (3584, 4096)]
+SCH = []
+DCH = [(0, 128), (128, 256)]
+KS = (0, 1, 2, 3)
+CYC, CG, FIX, SFIX, WAKE, PEC = 0.00083, 1.5, 0.04, 0.06, 0.07, 0.00042
+
+
+def rank_program(g, core, T, topo):
+    rank = T.rank_of(core)
+    if rank is None:
+        return
+    Q = {"v": g.vector, "s": g.scalar, "t": g.tensor, "g": g, "y": g.sync}
+    SEM = {"v": "sv", "s": "ss", "t": "st", "g": "sg"}
+    know = {q: {} for q in Q}
+    cnt, snap, log, nd = {}, {}, {}, [0]
+    prog = []
+
+    def a(n, lo=0, hi=None, st=1, r=None, r0=0):
+        if n in VIEW:
+            b, c, w = VIEW[n]
+            return a(b, c + lo, c + (w if hi is None else hi), st, r, r0)
+        return (n, lo, SCRATCH[n][1][1] if hi is None else hi, st, r0, SCRATCH[n][1][0] if r is None else r)
+
+    def ind(w, o):
+        return ("@", w, o)
+
+    def ap(o):
+        if o[0] == "@":
+            return ap(o[1]).indirect(ap(o[2]))
+        if o[0] == "!":
+            return o[1]
+        b = T[o[0]]
+        return b[o[4]:o[5], o[1]:o[2]] if o[3] == 1 else b[o[4]:o[5], o[1]:o[2]:o[3]]
+
+    def parts(o):
+        return [o[1], o[2]] if o[0] == "@" else [] if o[0] == "!" else [o]
+
+    def flat(reads, writes):
+        return [(k, p) for k, ops in (("r", reads), ("w", writes)) for o in ops for p in parts(o)]
+
+    def size(o):
+        return (o[2][2] - o[2][1]) * 16 if o[0] == "@" else (o[2] - o[1] + o[3] - 1) // o[3]
+
+    def meets(q, acc, lg):
+        for kind, (n, lo, hi, st, r0, r1) in acc:
+            for e in lg.get(n, []):
+                if n in PSUM and e[4] != q:
+                    yield e, kind
+                elif lo < e[1] and e[0] < hi and "w" in (kind, e[2]):
+                    yield e, kind
+                elif n in PSUM and q == "t" and kind == "w" and e[2] == "w":
+                    yield e, kind
+
+    def note(q, acc, lg, ref):
+        for kind, (n, lo, hi, st, r0, r1) in acc:
+            old = lg.get(n, [])
+            if kind == "w" and st == 1 and n not in PSUM:
+                old = [e for e in old if not (lo <= e[0] and e[1] <= hi)]
+            if n in PSUM and kind == "w":
+                old = [e for e in old if e[4] == q and not (kind == "w" and st == 1 and lo <= e[0] and e[1] <= hi)]
+            lg[n] = old + [(lo, hi, kind, ref, q)]
+
+    def add(q, call, reads, writes, dur, lat=0.0, kind="c", extra=None):
+        prog.append({"q": q, "call": call, "acc": flat(reads, writes), "dur": dur, "lat": lat, "kind": kind, "extra": extra})
+
+    def vcost(o, ins, two=False):
+        n = max(size(x) for x in ins)
+        if any(x[0] == "@" for x in ins):
+            return FIX + CYC * CG * n
+        f = 2.0 if two and not any(x[0] in PSUM for x in ins) else 1.0
+        return FIX + CYC * max(64, n * f)
+
+    def tt(o, x, y, op):
+        add("v", lambda: g.vector.tensor_tensor(ap(o), ap(x), ap(y), op), [x, y], [o], vcost(o, [x, y], True))
+
+    def ts(o, x, s1, op0, s2=None, op1=None):
+        rd = [x] + ([s1] if isinstance(s1, tuple) else [])
+
+        def call():
+            v1 = ap(s1) if isinstance(s1, tuple) else s1
+            if op1 is None:
+                return g.vector.tensor_scalar(ap(o), ap(x), v1, None, op0)
+            return g.vector.tensor_scalar(ap(o), ap(x), v1, s2, op0, op1)
+        add("v", call, rd, [o], vcost(o, [x]))
+
+    def cp(o, x):
+        add("v", lambda: g.vector.tensor_copy(ap(o), ap(x)), [x], [o], vcost(o, [x]))
+
+    def fill(o, c):
+        add("v", lambda: g.vector.memset(ap(o), c), [], [o], vcost(o, [o]))
+
+    def scan(o, d0, d1, op0, op1):
+        add("v", lambda: g.vector.tensor_tensor_scan(ap(o), ap(d0), ap(d1), 0.0, op0, op1), [d0, d1], [o], vcost(o, [d1]))
+
+    def act(o, x, func, scale=1.0, bias=0.0):
+        rd = [x] + ([scale] if isinstance(scale, tuple) else [])
+
+        def call():
+            return g.scalar.activation(ap(o), ap(x), func, bias, ap(scale) if isinstance(scale, tuple) else scale)
+        add("s", call, rd, [o], SFIX + CYC * size(x) * (CG if x[0] == "@" else 1.0))
+
+    def mm(o, l, r, start=True, stop=True):
+        w = 4 if SCRATCH[l[0]][2] == F32 else 1
+        add("t", lambda: g.tensor.matmul(ap(o), ap(l), ap(r), start, stop), [l, r], [o], 0.03 + PEC * w * max(min(64, size(l)), size(r)))
+
+    def tr(o, x, i):
+        add("t", lambda: g.tensor.transpose(ap(o), ap(x), ap(i)), [x, i], [o], 0.3)
+
+    def iota(o, pat, base, cmul):
+        def call():
+            if SCRATCH[o[0]][2] == I32:
+                return g.iota(ap(o), pat, base, cmul)
+            return g.iota(ap(o), pat, base, cmul, allow_small_or_imprecise_dtypes=True)
+        add("g", call, [], [o], 0.15 + 2 * CYC * size(o))
+
+    def dma(q, out, in_, lat=2.0):
+        add(q, lambda: Q[q].dma_start(ap(out), ap(in_)), [in_], [out], 0.1, lat, "d")
+
+    def dr(x):
+        return ("!", x)
+
+    def send(dst, src, to, rsem):
+        def call():
+            rid, pid, _ = topo.addr(to)
+            g.remote_dma(ap(dst), ap(src), T.sem[rsem], T.sem["rl"], pid, rid, topo.mask(core, to))
+        add("g", call, [src], [], 0.6, 0.0, "r", (rsem, len(topo.engines(core, to))))
+        prog[-1]["fly"] = len(prog)
+        add("net", None, [], [dst], 0.0, 2.2 + 0.3 * size(dst) / 256, "n", (rsem, len(topo.engines(core, to)), len(prog) - 1))
+
+    dma("y", a("ini", 0, 256), dr(T.gs[:]))
+    dma("s", a("ini", 256, 512), dr(T.gf[:]))
+    dma("y", a("ini", 512, 768), dr(T.gcl[:]))
+    dma("s", a("fri"), dr(T.fr[:]))
+    NS = 4
+    for j in range(NS):
+        w = 4096 // NS
+        dma("ys"[j % 2], a("ski", w * j, w * j + w), dr(T.sk[:, w * j:w * j + w]), 3.0 + 1.5 * j)
+    dma("s", a("xr", 592, 4096), dr(T.x[:, 0:3504]), 11.0)
+    dma("y", a("xr", 0, 592), dr(T.x[:, 3504:4096]), 11.0)
+    dma("y", a("thi", 0, 1), dr(T.th[:]), 11.0)
+    iota(a("ci"), [[1, 256]], 0, 0)
+    iota(a("pi"), [[0, 256]], 0, 1)
+    iota(a("il"), [[128, 2], [0, 8]], 16, 1)
+    iota(a("tabb", 0, 512), [[1, 512]], 16, 0)
+    iota(a("tabb", 512, 768), [[1, 256]], 16, 0)
+    iota(a("cm"), [[0, 16], [1, 16]], 0, 0)
+    iota(a("tabh", 0, 512), [[0, 512]], 0, 0)
+    iota(a("tabh", 512, 768), [[0, 256]], 1, 0)
+    iota(a("onef"), [[0, 128]], 1, 0)
+    iota(a("oneb"), [[0, 128]], 1, 0)
+    iota(a("eight"), [[0, 16]], 8, 0)
+    iota(a("lim"), [[0, 16]], 8, 0)
+    iota(a("krow", 0, 128, 1, 1), [[0, 8], [-1, 16]], 16, 0)
+    tt(a("idf"), a("pi", 0, 128), a("ci", 0, 128), OP.is_equal)
+    cp(a("idb"), a("idf"))
+    ts(a("idk"), a("idf"), 8192, OP.mult)
+    ts(a("ps"), a("pi", 0, 8), 4, OP.arith_shift_right)
+    tt(a("j8"), a("ps"), a("ci", 0, 8), OP.is_equal)
+    ts(a("pm"), a("pi"), 15, OP.bitwise_and)
+    tt(a("mske"), a("pm"), a("cm"), OP.is_equal)
+    cp(a("el"), a("ci", 0, 16))
+    ts(a("inf", 0, 256), a("ini", 0, 256), 1024, OP.mult, 16, OP.add)
+    ts(a("inf", 256, 512), a("ini", 512, 768), 1024, OP.mult, 16, OP.add)
+    tt(a("ine", 0, 256), a("inf", 0, 256), a("ini", 256, 512), OP.add)
+    tt(a("ine", 256, 512), a("inf", 256, 512), a("ci", 0, 256, 1, 8), OP.add)
+    for x in H:
+        for ch in H:
+            mm(a("pl", 16 * x + 8 * ch, 16 * x + 8 * ch + 8), a("ine", 256 * x + 128 * ch, 256 * x + 128 * ch + 128), a("idf", 0, 8, 1, 8))
+    cp(a("lsb"), a("pl", 0, 32))
+    mkA, keep, emhi, eg0, em = a("b1", 0, 256), a("b1", 256, 512), a("b0", 0, 256), a("b0", 256, 512), a("pe", 256, 512)
+    tmp, fx = keep, emhi
+
+    def to_w(x):
+        tt(a("lh", 256 * x, 256 * x + 256), ind(a("lsb", 16 * x, 16 * x + 16), a("el")), a("mske"), OP.mult)
+        for ch in H:
+            mm(a("pl", 64 + 16 * x + 8 * ch, 72 + 16 * x + 8 * ch), a("lh", 256 * x + 128 * ch, 256 * x + 128 * ch + 128), a("j8"))
+
+    def upper(o, x):
+        ts(o, x, 1.0 / 1024, OP.mult, -1.0 / 64, OP.add)
+
+    def lists(t):
+        ts(a("wi"), a("pl", 64, 96), -16, OP.add)
+        ts(a("wq"), a("wi"), 1023, OP.bitwise_and)
+        cp(a("fl"), a("wq", 0, 16))
+        upper(a("sl", 32 * t, 32 * t + 32), a("pl", 64, 96))
+
+    def clause_lists():
+        tt(a("we"), a("wq", 16, 32), a("iw"), OP.is_equal)
+        ts(a("wf"), a("we"), 512, OP.mult)
+        tt(a("wh"), a("wf"), a("wq", 16, 32), OP.add)
+        cp(a("hl"), a("wh"))
+        act(a("hi"), ind(a("tabh"), a("hl")), AF.Identity)
+        act(a("hb"), ind(a("tabb"), a("hl")), AF.Identity)
+
+    def next_saved():
+        upper(a("s3"), a("sv"))
+        tt(a("t4"), a("s3", 0, 16), a("s3", 16, 32), OP.mult)
+        ts(a("t8"), a("s3", 16, 32), 1, OP.add)
+        ts(a("t5"), a("t4"), 5, OP.arith_shift_right)
+        tt(a("t6"), a("t5"), a("t8"), OP.add)
+        ts(a("t7"), a("t6"), 4095, OP.bitwise_and)
+        ts(a("t1"), a("t7"), 1024, OP.mult)
+        tt(a("st"), a("t1"), a("il"), OP.add)
+
+    def own_parts(F):
+        act(em, a(F, 0, 256), AF.Relu, -1.0, 1.0)
+        act(a("f3p"), a(F, 0, 256), AF.Relu, 1.0, -float(U))
+        act(a("own3"), a("f3p"), AF.Identity, 1.0, float(U))
+
+    ts(a("wf"), a("ci", 0, 16), 16, OP.mult)
+    tt(a("iw"), a("wf"), a("pm", 0, 16), OP.add)
+    to_w(0)
+    to_w(1)
+    lists(4)
+    clause_lists()
+    act(a("fb"), ind(a("tabb", 0, 512), a("fl")), AF.Identity)
+    ts(a("frs"), a("fri"), 9, OP.arith_shift_right)
+    ts(tmp, a("frs"), 512, OP.mult, 16 + U, OP.add)
+    tt(a("x3"), a("fri"), tmp, OP.add)
+    ts(a("frm"), a("fri"), 0, OP.is_ge)
+    tt(a("f0", 0, 256), a("x3"), a("frm"), OP.mult)
+    ts(mkA, a("frm"), 2, OP.mult)
+    act(a("f0", 256, 512), a("f0", 0, 256), AF.Identity)
+    own_parts("f0")
+    for j in range(8):
+        s = 512 * j
+        if j in KS:
+            h = a(("pr", "sr")[j % 2])
+            cp(a("skv", s, s + 512), a("ski", s, s + 512))
+            act(a("sks", s, s + 512), a("skv", s, s + 512), AF.Sign, -1.0, 4095.5)
+            mm(h, a("idf"), a("skv", s, s + 512), True, False)
+            mm(h, a("idk"), a("sks", s, s + 512), False, True)
+            act(a("skt", s, s + 512), h, AF.Identity, 1024.0, float(U))
+            continue
+        h = a(("d0", "d1")[j % 2])
+        ts(h, a("ski", s, s + 512), 4096, OP.is_lt, 16384, OP.mult)
+        tt(a("skv", s, s + 512), a("ski", s, s + 512), h, OP.add)
+        act(a("skt", s, s + 512), a("skv", s, s + 512), AF.Identity, 1024.0, -float(U))
+    ts(a("b16"), a("j8"), 16, OP.mult)
+    ts(a("nidb"), a("idb"), -1, OP.mult)
+    ts(a("k0"), a("pm", 0, 8), 0, OP.is_equal)
+    ts(a("rst"), a("cm"), 0, OP.not_equal)
+    ts(a("thf", 0, 1), a("thi", 0, 1), 16, OP.mult, 16, OP.add)
+    ts(a("dg"), a("idf"), a("thf", 0, 1), OP.mult)
+    mm(a("pr", 0, 128), a("onef"), a("dg"))
+    for ch in H:
+        cp(a("thrt", 128 * ch, 128 * ch + 128), a("pr", 0, 128))
+    ts(a("thj", 0, 1), a("thi", 0, 1), -1, OP.add)
+    ts(a("thj", 1, 2), a("thj", 0, 1), 1, OP.arith_shift_right)
+    ts(a("thf", 1, 2), a("thj", 1, 2), 16, OP.mult, 16, OP.add)
+    cp(a("sv"), a("lsb"))
+    next_saved()
+
+    def places(raw, m, p, q, pr, r, u):
+        ts(a(m), a(raw), U - 1, OP.bitwise_and)
+        ts(a(q), a(raw), 1023, OP.bitwise_and)
+        ts(a(p), a(m), 1.0 / 1024, OP.mult, 592 - 1.0 / 64, OP.add)
+        tt(a(pr), a(p), a(q), OP.mult)
+        ts(a(r), a(pr), 4, OP.arith_shift_right, 4095, OP.bitwise_and)
+        cp(a(u), a(r))
+
+    for t in range(RO):
+        F, last = "f%d" % t, t == RO - 1
+        b = 32 * ((t + 4) % 5)
+        if t == 0:
+            tt(a("tg"), ind(a("skt"), a("sl", b, b + 16)), a("fb"), OP.add)
+            tt(a("rawg"), ind(a(F, 0, 512), a("fl")), a("tg"), OP.max)
+        else:
+            tt(a("tg"), ind(a("skt"), a("sarr", 16 * t, 16 * t + 16)), a("tabb", 256, 512), OP.add)
+            tt(a("rawg"), a(F, 256, 512), a("tg"), OP.max)
+        places("rawg", "ga", "pg", "qg", "prg", "rg", "ug")
+        for lo, hi in GCH:
+            act(a("ub", lo, hi), ind(a("xr"), a("ug", lo // 16, hi // 16)), AF.Identity)
+        tt(emhi, a("hi"), em, OP.mult)
+        tt(a("tc"), ind(a("skt"), a("sl", b + 16, b + 32)), a("hb"), OP.add)
+        tt(eg0, emhi, a("ga"), OP.mult)
+        tt(a(F, 512, 768), a("own3"), eg0, OP.add)
+        tt(a("rawc"), ind(a(F), a("hl")), a("tc"), OP.max)
+        places("rawc", "ca", "pc", "qc", "prc", "rc", "uc")
+        for j, (lo, hi) in enumerate(SCH):
+            d = a("d%d" % (j % 2))
+            act(a("wb", lo, hi), ind(a("xr"), a("uc", lo // 16, hi // 16)), AF.Identity)
+            mm(d, a("idb"), a("ub", lo, hi), True, False)
+            mm(d, a("nidb"), a("wb", lo, hi), False, True)
+            act(a("ab", lo, hi), d, AF.Abs)
+        for lo, hi in VCH:
+            tt(a("df", lo, hi), ind(a("xr"), a("uc", lo // 16, hi // 16)), a("ub", lo, hi), OP.subtract)
+            act(a("ab", lo, hi), a("df", lo, hi), AF.Abs)
+        for ch in H:
+            mm(a("pe", 128 * ch, 128 * ch + 128), a("oneb", 0, 128, 1, 1), a("krow", 0, 128, 1, 1), True, False)
+            for lo, hi in DCH:
+                if lo // 128 == ch:
+                    for k in range(16):
+                        mm(a("pe", 128 * ch + k, 128 * ch + 128, 16, hi - 128 * ch, lo - 128 * ch), a("ab", 16 * lo + k, 16 * hi, 16), a("b16"), False, k == 15 and hi % 128 == 0)
+        tt(a("fr5"), a("rawc"), a(F, 512, 768), OP.is_equal)
+        tt(fx, a("fr5"), eg0, OP.mult)
+        tt(a("x3"), a("own3"), fx, OP.add)
+        tt(a("mk2"), a("fr5"), mkA, OP.max)
+        tt(a("nov"), a("pe", 0, 256), a("thrt"), OP.is_le)
+        tt(a("key"), a("nov"), a("pe", 0, 256), OP.mult)
+        scan(a("cnt"), a("rst"), a("nov"), OP.mult, OP.add)
+        scan(a("sm"), a("rst"), a("key"), OP.mult, OP.max)
+        tt(a("cl"), a("cnt", 15, 256, 16), a("lim"), OP.is_le)
+        tt(a("smx"), a("sm", 15, 256, 16), a("cl"), OP.add)
+        act(a("lhb", 0, 256), ind(a("cl"), a("el")), AF.Identity)
+        tt(a("sel"), ind(a("smx"), a("el")), a("key"), OP.is_equal)
+        for ch in H:
+            mm(a("sr", 128 * ch, 128 * ch + 128), a("sel", 128 * ch, 128 * ch + 128), a("idb"))
+        for ch in H:
+            mm(a("pr", 128 * ch, 128 * ch + 128), a("lhb", 128 * ch, 128 * ch + 128), a("idb"))
+        for ch in H:
+            mm(a("pr", 256 + 128 * ch, 384 + 128 * ch), a("sel", 128 * ch, 128 * ch + 128), a("idb"))
+        tt(a("clst", 0, 16), a("cl"), a("sv", 0, 16), OP.mult)
+        tt(a("clst", 16, 32), a("cl"), a("st"), OP.mult)
+        tt(a("pgc", 0, 256), a("ga"), a("sr", 0, 256), OP.mult)
+        tt(a("pgc", 256, 512), a("ca"), a("sr", 0, 256), OP.mult)
+        act(a("thp"), a("pr", 256, 512), AF.Copy, a("thf", 1, 2))
+        mm(a("pl", 0, 32), a("idf"), a("clst"), True, False)
+        for x in H:
+            for ch in H:
+                mm(a("pl", 16 * x + 8 * ch, 16 * x + 8 * ch + 8), a("pgc", 256 * x + 128 * ch, 256 * x + 128 * ch + 128), a("j8"), False, x + ch == 2)
+        tt(keep, a("mk2"), a("pr", 0, 256), OP.is_gt)
+        tt(a("oi") if last else a(F, 0, 256), a("x3"), keep, OP.mult)
+        cp(a("lsb"), a("pl", 0, 32))
+        if not last:
+            to = T.cores[(rank + 1 + t % 3) % N]
+            to_w(0)
+            to_w(1)
+            lists(t)
+            send(a("sarr", 16 * t + 16, 16 * t + 32), a("sl", 32 * t, 32 * t + 16), to, "as%d" % t)
+            act(a("snd%d" % t), ind(a(F, 0, 512), a("fl")), AF.Identity)
+            send(a("f%d" % (t + 1), 256, 512), a("snd%d" % t), to, "ac%d" % t)
+        for ch in H:
+            mm(a("pl", 32 + 8 * ch, 40 + 8 * ch), a("thp", 128 * ch, 128 * ch + 128), a("j8"))
+        tt(a("ns"), a("smx"), a("pl", 32, 48), OP.is_gt)
+        if not last:
+            clause_lists()
+            own_parts(F)
+            act(a("f%d" % (t + 1), 0, 256), a(F, 0, 256), AF.Identity)
+        act(a("lhb", 256, 512), ind(a("ns"), a("el")), AF.Identity)
+        ts(a("sc", 0, 16), a("ns"), -1, OP.mult, 1, OP.add)
+        tt(a("s1"), a("lsb"), a("sv"), OP.subtract)
+        tt(a("sc", 16, 32), a("sc", 0, 16), a("cl"), OP.add)
+        tt(a("s2"), a("s1"), a("sc"), OP.mult)
+        tt(a("sv"), a("sv"), a("s2"), OP.add)
+        for ch in H:
+            mm(a("pr", 256 + 128 * ch, 384 + 128 * ch), a("lhb", 256 + 128 * ch, 384 + 128 * ch), a("idb"))
+        if not last:
+            act(a("rcb"), a("pr", 0, 256), AF.Copy)
+            for ch in H:
+                mm(a("pl", 48 + 8 * ch, 56 + 8 * ch), a("rcb", 128 * ch, 128 * ch + 128), a("k0"))
+            next_saved()
+        tt(a("eqm"), a("mk2"), a("pr", 256, 512), OP.is_gt)
+        if last:
+            break
+        tt(mkA, keep, a("eqm"), OP.add)
+        cp(a("pai"), a("pl", 48, 64))
+        ts(a("paj"), a("pai"), 1, OP.bitwise_and)
+        tt(a("lim"), a("eight"), a("paj"), OP.subtract)
+
+    ts(a("op"), a("oi"), 10, OP.arith_shift_right, 4095, OP.bitwise_and)
+    ts(mkA, a("op"), -512, OP.mult, -16 - U, OP.add)
+    tt(a("oy"), a("oi"), mkA, OP.add)
+    tt(a("oy2"), keep, a("eqm"), OP.subtract)
+    ts(mkA, a("oy"), 2, OP.mult, -1, OP.max)
+    tt(a("oz"), a("oy2"), mkA, OP.add)
+    dma("y", dr(T.yf[:]), a("oz"))
+    cp(a("fin", 0, 32), a("lsb"))
+    cp(a("fin", 32, 64), a("sv"))
+    upper(a("fip"), a("fin"))
+    ts(a("fiq", 0, 48), a("fip", 0, 48), -512, OP.mult, -16, OP.add)
+    tt(a("fim", 0, 48), a("fin", 0, 48), a("fiq", 0, 48), OP.add)
+    cp(a("fim", 48, 64), a("fip", 48, 64))
+    tr(a("pl", 0, 128, 1, 64), a("fim"), a("idf"))
+    cp(a("fot"), a("pl", 0, 128, 1, 64))
+    for j, y in enumerate((T.yg, T.yc, T.ysg, T.yk)):
+        for ch in H:
+            r0 = 16 * j + 8 * ch
+            dma("ys"[(2 * j + ch) % 2], dr(y[:, 128 * ch:128 * ch + 128]), a("fot", 0, 128, 1, r0 + 8, r0))
+
+    lg, n = {}, len(prog)
+    dep, succ = [[] for _ in range(n)], [[] for _ in range(n)]
+    for i, p in enumerate(prog):
+        ds = {}
+        for e, kind in meets(p["q"] if p["kind"] == "c" else "#%d" % i, p["acc"], lg):
+            ds[e[3]] = 0.0 if (p["q"] == "t" and prog[e[3]]["q"] == "t") else WAKE
+        if p["kind"] == "n":
+            ds[p["extra"][2]] = 0.0
+        note(p["q"] if p["kind"] == "c" else "#%d" % i, p["acc"], lg, i)
+        dep[i] = sorted(ds.items())
+        for d, w in dep[i]:
+            succ[d].append((i, w))
+    rankp = [0.0] * n
+    for i in range(n - 1, -1, -1):
+        p = prog[i]
+        rankp[i] = p["dur"] + p["lat"] + max([w + rankp[j] for j, w in succ[i]] + [0.0])
+    free = {q: 0.0 for q in list(Q) + ["net"]}
+    left = [len(d) for d in dep]
+    done = [0.0] * n
+    ready = {q: [] for q in free}
+    for i in range(n):
+        if not left[i]:
+            ready[prog[i]["q"]].append((0.0, i))
+    plan = []
+    for _ in range(n):
+        best = None
+        for q in free:
+            if not ready[q]:
+                continue
+            t0 = max(free[q], min(e for e, i in ready[q])) if q != "net" else min(e for e, i in ready[q])
+            c = max(((rankp[i], -i) for e, i in ready[q] if e <= t0 + 1e-9))
+            i = -c[1]
+            if best is None or t0 < best[0]:
+                best = (t0, i, q)
+        t0, i, q = best
+        ready[q] = [x for x in ready[q] if x[1] != i]
+        if q != "net":
+            free[q] = t0 + prog[i]["dur"]
+        done[i] = t0 + prog[i]["dur"] + prog[i]["lat"]
+        plan.append(i)
+        for j, w in succ[i]:
+            left[j] -= 1
+            if not left[j]:
+                ready[prog[j]["q"]].append((max(done[d] + w2 for d, w2 in dep[j]), j))
+
+    def wait(q, sem, c):
+        if know[q].get(sem, 0) < c:
+            Q[q].wait_ge(T.sem[sem], c)
+            for k, v in snap.get((sem, c), {}).items():
+                know[q][k] = max(know[q].get(k, 0), v)
+            know[q][sem] = c
+
+    ref = {}
+    for i in plan:
+        p = prog[i]
+        q = p["q"]
+        if p["kind"] != "n":
+            want = {}
+            for d, w in dep[i]:
+                if q == "t" and prog[d]["q"] == "t":
+                    continue
+                sem, c = ref[d]
+                want[sem] = max(want.get(sem, 0), c)
+            for sem in sorted(want, key=lambda s: (s == SEM.get(q), s)):
+                wait(q, sem, want[sem])
+            inst = p["call"]()
+        if p["kind"] == "c":
+            sem = SEM[q]
+            inst.then_inc(T.sem[sem], 1)
+            cnt[sem] = cnt.get(sem, 0) + 1
+        elif p["kind"] == "d":
+            sem = "d%d" % nd[0]
+            nd[0] += 1
+            inst.then_inc(T.sem[sem], 16)
+            cnt[sem] = 16
+        elif p["kind"] == "r":
+            sem = "rl"
+            cnt[sem] = cnt.get(sem, 0) + p["extra"][1]
+        else:
+            sem = p["extra"][0]
+            cnt[sem] = p["extra"][1]
+        ref[i] = (sem, cnt[sem])
+        if p["kind"] != "n":
+            snap[ref[i]] = dict(know[q])
+    for sem in sorted(cnt):
+        g.wait_ge(T.sem[sem], cnt[sem])

@@ -17,12 +17,12 @@ def _bufs(where, dtype, text):
 
 
 _bufs("sbuf", F32, "skv:4096 skt:4096 inf:8x512 ine:8x512 thf:8 tabb:768 tabh:768 j8:8 mske:256 rst:256 idf:128 onef:128 thrt:256 "
-      "iw:16 il:16 eight:16 lim:16 fb:256 hb:256 hi:256 tg:256 tc:256 f3p:256 own3:256 x3:256 eqm:256 nov:256 key:256 cnt:256 sm:256 "
-      "cl:16 smx:16 pgc:512 thp:256 st:16 clst:32 lsb:32 lh:512 we:16 wf:16 wh:16 sc:32 ns:16 sv:32 s1:32 s2:32 t1:16 "
+      "iw:16 il:16 lim:16 fb:256 hb:256 tg:256 tc:256 f3p:256 own3:256 x3:256 eqm:256 nov:256 key:256 cnt:256 sm:256 "
+      "cl:16 smx:16 pgc:512 thp:256 clst:32 lsb:32 lh:512 we:16 wf:16 wh:16 sc:32 sv:32 s1:32 s2:32 t1:16 st:16 par:64 "
       "fot:64x128 oy:256 oy2:256 oz:256 f0:768 f1:768 f2:768 f3:768 f4:768 snd0:256 snd1:256 snd2:256 snd3:256")
-_bufs("sbuf", BF, "idk:128 xr:4096 ub:4096 wb:4096 df:4096 ab:4096 b16:8 idb:128 nidb:128 k0:8 rcb:256 oneb:128 krow:128 fr5:256 mk2:256 sel:256 lhb:512")
+_bufs("sbuf", BF, "idk:128 xr:4096 ub:4096 hi:256 em:256 df:4096 ab:4096 b16:8 idb:128 k0:8 zero:16 rcb:256 oneb:128 krow:128 fr5:256 mk2:256 sel:256 lhb:512")
 _bufs("sbuf", I32, "ski:4096 ini:8x768 fri:256 thi:8 thj:8 pi:256 ci:256 pm:256 cm:256 ps:8 rawg:256 rawc:256 ga:256 ca:256 "
-      "pg:256 qg:256 prg:256 rg:256 pc:256 qc:256 prc:256 rc:256 wi:32 wq:32 pai:16 paj:16 s3:32 t4:16 t5:16 t6:16 t7:16 t8:16 fip:64 oi:256 op:256")
+      "pg:256 qg:256 prg:256 rg:256 pc:256 qc:256 prc:256 rc:256 wi:32 wq:32 s3:32 t4:16 t5:16 t6:16 t7:16 t8:16 fip:64 oi:256 op:256")
 _bufs("sbuf", U16, "ug:256 uc:256 el:16 fl:16 hl:16 sl:160 sarr:80")
 _bufs("psum", F32, "b0:512 b1:512 pe:512 pl:512 pr:512 sr:512 d0:512 d1:512")
 SEMAPHORES = ["sv", "ss", "st", "sg", "rl"] + ["as%d" % t for t in range(4)] + ["ac%d" % t for t in range(4)] + ["d%d" % t for t in range(24)]
@@ -30,10 +30,10 @@ VIEW = {"sks": ("df", 0, 4096), "frs": ("op", 0, 256), "frm": ("oy", 0, 256), "d
 PSUM = [n for n in SCRATCH if SCRATCH[n][0] == "psum"]
 GCH = [(0, 1024), (1024, 2048), (2048, 3072), (3072, 4096)]
 VCH = [(0, 1024), (1024, 2048), (2048, 3072), (3072, 3584), (3584, 4096)]
-SCH = []
-DCH = [(0, 128), (128, 256)]
-KS = (0, 1, 2, 3)
-CYC, CG, FIX, SFIX, WAKE, PEC = 0.00083, 1.5, 0.04, 0.06, 0.07, 0.00042
+PH = [(0, 128), (128, 256)]
+KS = (0, 2, 4)
+CYC, CG, FIX, GFIX, SFIX, WAKE, PEC = 0.00083, 1.5, 0.01, 0.05, 0.06, 0.11, 0.00071
+SLACK, OVER, UP, UQ = 0.1, 0.05, 1.5, 3.0
 
 
 def rank_program(g, core, T, topo):
@@ -43,8 +43,8 @@ def rank_program(g, core, T, topo):
     Q = {"v": g.vector, "s": g.scalar, "t": g.tensor, "g": g, "y": g.sync}
     SEM = {"v": "sv", "s": "ss", "t": "st", "g": "sg"}
     know = {q: {} for q in Q}
-    cnt, snap, log, nd = {}, {}, {}, [0]
-    prog = []
+    cnt, snap, nd = {}, {}, [0]
+    prog, boost = [], [0.0]
 
     def a(n, lo=0, hi=None, st=1, r=None, r0=0):
         if n in VIEW:
@@ -88,16 +88,16 @@ def rank_program(g, core, T, topo):
             if kind == "w" and st == 1 and n not in PSUM:
                 old = [e for e in old if not (lo <= e[0] and e[1] <= hi)]
             if n in PSUM and kind == "w":
-                old = [e for e in old if e[4] == q and not (kind == "w" and st == 1 and lo <= e[0] and e[1] <= hi)]
+                old = [e for e in old if e[4] == q and not (st == 1 and lo <= e[0] and e[1] <= hi)]
             lg[n] = old + [(lo, hi, kind, ref, q)]
 
     def add(q, call, reads, writes, dur, lat=0.0, kind="c", extra=None):
-        prog.append({"q": q, "call": call, "acc": flat(reads, writes), "dur": dur, "lat": lat, "kind": kind, "extra": extra})
+        prog.append({"up": boost[0], "q": q, "call": call, "acc": flat(reads, writes), "dur": dur, "lat": lat, "kind": kind, "extra": extra})
 
     def vcost(o, ins, two=False):
         n = max(size(x) for x in ins)
         if any(x[0] == "@" for x in ins):
-            return FIX + CYC * CG * n
+            return GFIX + CYC * CG * n
         f = 2.0 if two and not any(x[0] in PSUM for x in ins) else 1.0
         return FIX + CYC * max(64, n * f)
 
@@ -105,20 +105,14 @@ def rank_program(g, core, T, topo):
         add("v", lambda: g.vector.tensor_tensor(ap(o), ap(x), ap(y), op), [x, y], [o], vcost(o, [x, y], True))
 
     def ts(o, x, s1, op0, s2=None, op1=None):
-        rd = [x] + ([s1] if isinstance(s1, tuple) else [])
-
         def call():
-            v1 = ap(s1) if isinstance(s1, tuple) else s1
             if op1 is None:
-                return g.vector.tensor_scalar(ap(o), ap(x), v1, None, op0)
-            return g.vector.tensor_scalar(ap(o), ap(x), v1, s2, op0, op1)
-        add("v", call, rd, [o], vcost(o, [x]))
+                return g.vector.tensor_scalar(ap(o), ap(x), s1, None, op0)
+            return g.vector.tensor_scalar(ap(o), ap(x), s1, s2, op0, op1)
+        add("v", call, [x], [o], vcost(o, [x]))
 
     def cp(o, x):
         add("v", lambda: g.vector.tensor_copy(ap(o), ap(x)), [x], [o], vcost(o, [x]))
-
-    def fill(o, c):
-        add("v", lambda: g.vector.memset(ap(o), c), [], [o], vcost(o, [o]))
 
     def scan(o, d0, d1, op0, op1):
         add("v", lambda: g.vector.tensor_tensor_scan(ap(o), ap(d0), ap(d1), 0.0, op0, op1), [d0, d1], [o], vcost(o, [d1]))
@@ -155,7 +149,6 @@ def rank_program(g, core, T, topo):
             rid, pid, _ = topo.addr(to)
             g.remote_dma(ap(dst), ap(src), T.sem[rsem], T.sem["rl"], pid, rid, topo.mask(core, to))
         add("g", call, [src], [], 0.6, 0.0, "r", (rsem, len(topo.engines(core, to))))
-        prog[-1]["fly"] = len(prog)
         add("net", None, [], [dst], 0.0, 2.2 + 0.3 * size(dst) / 256, "n", (rsem, len(topo.engines(core, to)), len(prog) - 1))
 
     dma("y", a("ini", 0, 256), dr(T.gs[:]))
@@ -179,12 +172,12 @@ def rank_program(g, core, T, topo):
     iota(a("tabh", 512, 768), [[0, 256]], 1, 0)
     iota(a("onef"), [[0, 128]], 1, 0)
     iota(a("oneb"), [[0, 128]], 1, 0)
-    iota(a("eight"), [[0, 16]], 8, 0)
+    iota(a("zero"), [[0, 16]], 0, 0)
     iota(a("lim"), [[0, 16]], 8, 0)
     iota(a("krow", 0, 128, 1, 1), [[0, 8], [-1, 16]], 16, 0)
     tt(a("idf"), a("pi", 0, 128), a("ci", 0, 128), OP.is_equal)
-    cp(a("idb"), a("idf"))
-    ts(a("idk"), a("idf"), 8192, OP.mult)
+    act(a("idb"), a("idf"), AF.Copy)
+    act(a("idk"), a("idf"), AF.Copy, 8192.0)
     ts(a("ps"), a("pi", 0, 8), 4, OP.arith_shift_right)
     tt(a("j8"), a("ps"), a("ci", 0, 8), OP.is_equal)
     ts(a("pm"), a("pi"), 15, OP.bitwise_and)
@@ -198,8 +191,8 @@ def rank_program(g, core, T, topo):
         for ch in H:
             mm(a("pl", 16 * x + 8 * ch, 16 * x + 8 * ch + 8), a("ine", 256 * x + 128 * ch, 256 * x + 128 * ch + 128), a("idf", 0, 8, 1, 8))
     cp(a("lsb"), a("pl", 0, 32))
-    mkA, keep, emhi, eg0, em = a("b1", 0, 256), a("b1", 256, 512), a("b0", 0, 256), a("b0", 256, 512), a("pe", 256, 512)
-    tmp, fx = keep, emhi
+    mkA, keep, emhi = a("b1", 0, 256), a("b1", 256, 512), a("pe", 256, 512)
+    pw = (a("pl", 64, 80), a("pl", 80, 96))
 
     def to_w(x):
         tt(a("lh", 256 * x, 256 * x + 256), ind(a("lsb", 16 * x, 16 * x + 16), a("el")), a("mske"), OP.mult)
@@ -209,19 +202,28 @@ def rank_program(g, core, T, topo):
     def upper(o, x):
         ts(o, x, 1.0 / 1024, OP.mult, -1.0 / 64, OP.add)
 
-    def lists(t):
-        ts(a("wi"), a("pl", 64, 96), -16, OP.add)
-        ts(a("wq"), a("wi"), 1023, OP.bitwise_and)
+    def goal_lists(t):
+        ts(a("wi", 0, 16), pw[0], -16, OP.add)
+        ts(a("wq", 0, 16), a("wi", 0, 16), 1023, OP.bitwise_and)
         cp(a("fl"), a("wq", 0, 16))
-        upper(a("sl", 32 * t, 32 * t + 32), a("pl", 64, 96))
+        upper(a("sl", 32 * t, 32 * t + 16), pw[0])
 
-    def clause_lists():
+    def clause_lists(t):
+        upper(a("sl", 32 * t + 16, 32 * t + 32), pw[1])
+        ts(a("wi", 16, 32), pw[1], -16, OP.add)
+        ts(a("wq", 16, 32), a("wi", 16, 32), 1023, OP.bitwise_and)
         tt(a("we"), a("wq", 16, 32), a("iw"), OP.is_equal)
         ts(a("wf"), a("we"), 512, OP.mult)
         tt(a("wh"), a("wf"), a("wq", 16, 32), OP.add)
         cp(a("hl"), a("wh"))
         act(a("hi"), ind(a("tabh"), a("hl")), AF.Identity)
         act(a("hb"), ind(a("tabb"), a("hl")), AF.Identity)
+
+    def clause_side(t):
+        tt(a("tc"), ind(a("skt"), a("sl", 32 * t + 16, 32 * t + 32)), a("hb"), OP.add)
+        mm(a("d1", 256, 512), a("idb"), a("hi"), True, False)
+        mm(a("d1", 256, 512), a("idb"), a("em"), False, True)
+        act(emhi, a("d1", 256, 512), AF.Relu, 1.0, -1.0)
 
     def next_saved():
         upper(a("s3"), a("sv"))
@@ -234,20 +236,20 @@ def rank_program(g, core, T, topo):
         tt(a("st"), a("t1"), a("il"), OP.add)
 
     def own_parts(F):
-        act(em, a(F, 0, 256), AF.Relu, -1.0, 1.0)
+        act(a("em"), a(F, 0, 256), AF.Relu, -1.0, 1.0)
         act(a("f3p"), a(F, 0, 256), AF.Relu, 1.0, -float(U))
         act(a("own3"), a("f3p"), AF.Identity, 1.0, float(U))
 
     ts(a("wf"), a("ci", 0, 16), 16, OP.mult)
     tt(a("iw"), a("wf"), a("pm", 0, 16), OP.add)
     to_w(0)
+    goal_lists(4)
     to_w(1)
-    lists(4)
-    clause_lists()
+    clause_lists(4)
     act(a("fb"), ind(a("tabb", 0, 512), a("fl")), AF.Identity)
     ts(a("frs"), a("fri"), 9, OP.arith_shift_right)
-    ts(tmp, a("frs"), 512, OP.mult, 16 + U, OP.add)
-    tt(a("x3"), a("fri"), tmp, OP.add)
+    ts(keep, a("frs"), 512, OP.mult, 16 + U, OP.add)
+    tt(a("x3"), a("fri"), keep, OP.add)
     ts(a("frm"), a("fri"), 0, OP.is_ge)
     tt(a("f0", 0, 256), a("x3"), a("frm"), OP.mult)
     ts(mkA, a("frm"), 2, OP.mult)
@@ -267,128 +269,138 @@ def rank_program(g, core, T, topo):
         ts(h, a("ski", s, s + 512), 4096, OP.is_lt, 16384, OP.mult)
         tt(a("skv", s, s + 512), a("ski", s, s + 512), h, OP.add)
         act(a("skt", s, s + 512), a("skv", s, s + 512), AF.Identity, 1024.0, -float(U))
-    ts(a("b16"), a("j8"), 16, OP.mult)
-    ts(a("nidb"), a("idb"), -1, OP.mult)
+    act(a("b16"), a("j8"), AF.Copy, 16.0)
     ts(a("k0"), a("pm", 0, 8), 0, OP.is_equal)
     ts(a("rst"), a("cm"), 0, OP.not_equal)
     ts(a("thf", 0, 1), a("thi", 0, 1), 16, OP.mult, 16, OP.add)
-    ts(a("dg"), a("idf"), a("thf", 0, 1), OP.mult)
+    act(a("dg"), a("idf"), AF.Copy, a("thf", 0, 1))
     mm(a("pr", 0, 128), a("onef"), a("dg"))
     for ch in H:
-        cp(a("thrt", 128 * ch, 128 * ch + 128), a("pr", 0, 128))
+        act(a("thrt", 128 * ch, 128 * ch + 128), a("pr", 0, 128), AF.Copy)
     ts(a("thj", 0, 1), a("thi", 0, 1), -1, OP.add)
     ts(a("thj", 1, 2), a("thj", 0, 1), 1, OP.arith_shift_right)
     ts(a("thf", 1, 2), a("thj", 1, 2), 16, OP.mult, 16, OP.add)
-    cp(a("sv"), a("lsb"))
+    act(a("sv"), a("lsb"), AF.Copy)
     next_saved()
 
     def places(raw, m, p, q, pr, r, u):
-        ts(a(m), a(raw), U - 1, OP.bitwise_and)
-        ts(a(q), a(raw), 1023, OP.bitwise_and)
-        ts(a(p), a(m), 1.0 / 1024, OP.mult, 592 - 1.0 / 64, OP.add)
-        tt(a(pr), a(p), a(q), OP.mult)
-        ts(a(r), a(pr), 4, OP.arith_shift_right, 4095, OP.bitwise_and)
-        cp(a(u), a(r))
+        for w in PH:
+            ts(a(m, *w), a(raw, *w), U - 1, OP.bitwise_and)
+            ts(a(q, *w), a(raw, *w), 1023, OP.bitwise_and)
+            ts(a(p, *w), a(m, *w), 1.0 / 1024, OP.mult, 592 - 1.0 / 64, OP.add)
+            tt(a(pr, *w), a(p, *w), a(q, *w), OP.mult)
+            ts(a(r, *w), a(pr, *w), 4, OP.arith_shift_right, 4095, OP.bitwise_and)
+            cp(a(u, *w), a(r, *w))
 
     for t in range(RO):
         F, last = "f%d" % t, t == RO - 1
         b = 32 * ((t + 4) % 5)
         if t == 0:
+            clause_side(4)
+        if t == 0:
             tt(a("tg"), ind(a("skt"), a("sl", b, b + 16)), a("fb"), OP.add)
             tt(a("rawg"), ind(a(F, 0, 512), a("fl")), a("tg"), OP.max)
         else:
             tt(a("tg"), ind(a("skt"), a("sarr", 16 * t, 16 * t + 16)), a("tabb", 256, 512), OP.add)
-            tt(a("rawg"), a(F, 256, 512), a("tg"), OP.max)
+            for lo, hi in PH:
+                tt(a("rawg", lo, hi), a(F, 256 + lo, 256 + hi), a("tg", lo, hi), OP.max)
+        boost[0] = UP
         places("rawg", "ga", "pg", "qg", "prg", "rg", "ug")
+        boost[0] = 0.0
         for lo, hi in GCH:
             act(a("ub", lo, hi), ind(a("xr"), a("ug", lo // 16, hi // 16)), AF.Identity)
-        tt(emhi, a("hi"), em, OP.mult)
-        tt(a("tc"), ind(a("skt"), a("sl", b + 16, b + 32)), a("hb"), OP.add)
-        tt(eg0, emhi, a("ga"), OP.mult)
-        tt(a(F, 512, 768), a("own3"), eg0, OP.add)
+        for lo, hi in PH:
+            e = a("b0", lo, hi)
+            tt(e, a("pe", 256 + lo, 256 + hi), a("ga", lo, hi), OP.mult)
+            tt(a(F, 512 + lo, 512 + hi), a("own3", lo, hi), e, OP.add)
         tt(a("rawc"), ind(a(F), a("hl")), a("tc"), OP.max)
         places("rawc", "ca", "pc", "qc", "prc", "rc", "uc")
-        for j, (lo, hi) in enumerate(SCH):
-            d = a("d%d" % (j % 2))
-            act(a("wb", lo, hi), ind(a("xr"), a("uc", lo // 16, hi // 16)), AF.Identity)
-            mm(d, a("idb"), a("ub", lo, hi), True, False)
-            mm(d, a("nidb"), a("wb", lo, hi), False, True)
-            act(a("ab", lo, hi), d, AF.Abs)
         for lo, hi in VCH:
             tt(a("df", lo, hi), ind(a("xr"), a("uc", lo // 16, hi // 16)), a("ub", lo, hi), OP.subtract)
             act(a("ab", lo, hi), a("df", lo, hi), AF.Abs)
         for ch in H:
-            mm(a("pe", 128 * ch, 128 * ch + 128), a("oneb", 0, 128, 1, 1), a("krow", 0, 128, 1, 1), True, False)
-            for lo, hi in DCH:
-                if lo // 128 == ch:
-                    for k in range(16):
-                        mm(a("pe", 128 * ch + k, 128 * ch + 128, 16, hi - 128 * ch, lo - 128 * ch), a("ab", 16 * lo + k, 16 * hi, 16), a("b16"), False, k == 15 and hi % 128 == 0)
-        tt(a("fr5"), a("rawc"), a(F, 512, 768), OP.is_equal)
-        tt(fx, a("fr5"), eg0, OP.mult)
-        tt(a("x3"), a("own3"), fx, OP.add)
+            D = ("d0", "d1")[ch]
+            mm(a(D, 0, 128), a("oneb", 0, 128, 1, 1), a("krow", 0, 128, 1, 1), True, False)
+            for k in range(16):
+                mm(a(D, k, 128, 16), a("ab", 2048 * ch + k, 2048 * ch + 2048, 16), a("b16"), False, k == 15)
+        mm(a("pr", 256, 512), a("idf"), a(F, 512, 768))
+        tt(a("fr5"), a("rawc"), a("pr", 256, 512), OP.is_equal)
         tt(a("mk2"), a("fr5"), mkA, OP.max)
-        tt(a("nov"), a("pe", 0, 256), a("thrt"), OP.is_le)
-        tt(a("key"), a("nov"), a("pe", 0, 256), OP.mult)
-        scan(a("cnt"), a("rst"), a("nov"), OP.mult, OP.add)
-        scan(a("sm"), a("rst"), a("key"), OP.mult, OP.max)
-        tt(a("cl"), a("cnt", 15, 256, 16), a("lim"), OP.is_le)
-        tt(a("smx"), a("sm", 15, 256, 16), a("cl"), OP.add)
-        act(a("lhb", 0, 256), ind(a("cl"), a("el")), AF.Identity)
-        tt(a("sel"), ind(a("smx"), a("el")), a("key"), OP.is_equal)
         for ch in H:
-            mm(a("sr", 128 * ch, 128 * ch + 128), a("sel", 128 * ch, 128 * ch + 128), a("idb"))
+            D, R = a(("d0", "d1")[ch], 0, 128), a(("sr", "pe")[ch], 0, 128)
+            lo, hi, l8 = 128 * ch, 128 * ch + 128, (8 * ch, 8 * ch + 8)
+            tt(a("nov", lo, hi), D, a("thrt", lo, hi), OP.is_le)
+            tt(a("key", lo, hi), a("nov", lo, hi), D, OP.mult)
+            scan(a("cnt", lo, hi), a("rst", lo, hi), a("nov", lo, hi), OP.mult, OP.add)
+            scan(a("sm", lo, hi), a("rst", lo, hi), a("key", lo, hi), OP.mult, OP.max)
+            tt(a("cl", *l8), a("cnt", lo + 15, hi, 16), a("lim", *l8), OP.is_le)
+            tt(a("smx", *l8), a("sm", lo + 15, hi, 16), a("cl", *l8), OP.add)
+            tt(a("sel", lo, hi), ind(a("smx", *l8), a("el", 0, 8)), a("key", lo, hi), OP.is_equal)
+            mm(R, a("sel", lo, hi), a("idb"))
+            tt(a("pgc", lo, hi), a("ga", lo, hi), R, OP.mult)
+            tt(a("pgc", 256 + lo, 256 + hi), a("ca", lo, hi), R, OP.mult)
+        act(a("lhb", 0, 256), ind(a("cl"), a("el")), AF.Identity)
         for ch in H:
             mm(a("pr", 128 * ch, 128 * ch + 128), a("lhb", 128 * ch, 128 * ch + 128), a("idb"))
+        tt(keep, a("mk2"), a("pr", 0, 256), OP.is_gt)
+        tt(a("oi") if last else a(F, 0, 256), a(F, 512, 768), keep, OP.mult)
+        if not last:
+            act(a("rcb"), a("pr", 0, 256), AF.Copy)
         for ch in H:
-            mm(a("pr", 256 + 128 * ch, 384 + 128 * ch), a("sel", 128 * ch, 128 * ch + 128), a("idb"))
+            act(a("thp", 128 * ch, 128 * ch + 128), a(("sr", "pe")[ch], 0, 128), AF.Copy, a("thf", 1, 2))
         tt(a("clst", 0, 16), a("cl"), a("sv", 0, 16), OP.mult)
         tt(a("clst", 16, 32), a("cl"), a("st"), OP.mult)
-        tt(a("pgc", 0, 256), a("ga"), a("sr", 0, 256), OP.mult)
-        tt(a("pgc", 256, 512), a("ca"), a("sr", 0, 256), OP.mult)
-        act(a("thp"), a("pr", 256, 512), AF.Copy, a("thf", 1, 2))
-        mm(a("pl", 0, 32), a("idf"), a("clst"), True, False)
         for x in H:
-            for ch in H:
-                mm(a("pl", 16 * x + 8 * ch, 16 * x + 8 * ch + 8), a("pgc", 256 * x + 128 * ch, 256 * x + 128 * ch + 128), a("j8"), False, x + ch == 2)
-        tt(keep, a("mk2"), a("pr", 0, 256), OP.is_gt)
-        tt(a("oi") if last else a(F, 0, 256), a("x3"), keep, OP.mult)
-        cp(a("lsb"), a("pl", 0, 32))
+            B, c = (("pl", 0), ("d1", 128))[x]
+            mm(a(B, c, c + 16), a("idb"), a("zero"), True, False)
+            mm(a(B, c, c + 8), a("pgc", 256 * x, 256 * x + 128), a("j8"), False, False)
+            mm(a(B, c, c + 16), a("idf"), a("clst", 16 * x, 16 * x + 16), False, False)
+            mm(a(B, c + 8, c + 16), a("pgc", 256 * x + 128, 256 * x + 256), a("j8"), False, True)
+            cp(a("lsb", 16 * x, 16 * x + 16), a(B, c, c + 16))
         if not last:
             to = T.cores[(rank + 1 + t % 3) % N]
             to_w(0)
-            to_w(1)
-            lists(t)
+            goal_lists(t)
             send(a("sarr", 16 * t + 16, 16 * t + 32), a("sl", 32 * t, 32 * t + 16), to, "as%d" % t)
             act(a("snd%d" % t), ind(a(F, 0, 512), a("fl")), AF.Identity)
             send(a("f%d" % (t + 1), 256, 512), a("snd%d" % t), to, "ac%d" % t)
+            to_w(1)
         for ch in H:
             mm(a("pl", 32 + 8 * ch, 40 + 8 * ch), a("thp", 128 * ch, 128 * ch + 128), a("j8"))
-        tt(a("ns"), a("smx"), a("pl", 32, 48), OP.is_gt)
         if not last:
-            clause_lists()
+            for ch in H:
+                mm(a("pl", 48 + 8 * ch, 56 + 8 * ch), a("rcb", 128 * ch, 128 * ch + 128), a("k0"))
+        tt(a("sc", 0, 16), a("smx"), a("pl", 32, 48), OP.is_le)
+        if not last:
+            clause_lists(t)
+            act(a("par", 0, 16), a("pl", 48, 64), AF.Abs, 1.0, -4.0)
+            act(a("par", 16, 32), a("par", 0, 16), AF.Abs, 1.0, -2.0)
+            act(a("par", 32, 48), a("par", 16, 32), AF.Abs, 1.0, -1.0)
+            act(a("lim"), a("par", 32, 48), AF.Identity, 1.0, 7.0)
             own_parts(F)
             act(a("f%d" % (t + 1), 0, 256), a(F, 0, 256), AF.Identity)
-        act(a("lhb", 256, 512), ind(a("ns"), a("el")), AF.Identity)
-        ts(a("sc", 0, 16), a("ns"), -1, OP.mult, 1, OP.add)
+            clause_side(t)
+        boost[0] = UQ
+        act(a("lhb", 256, 512), ind(a("sc", 0, 16), a("el")), AF.Identity, -1.0, 1.0)
+        boost[0] = 0.0
         tt(a("s1"), a("lsb"), a("sv"), OP.subtract)
         tt(a("sc", 16, 32), a("sc", 0, 16), a("cl"), OP.add)
         tt(a("s2"), a("s1"), a("sc"), OP.mult)
         tt(a("sv"), a("sv"), a("s2"), OP.add)
+        boost[0] = UQ
         for ch in H:
             mm(a("pr", 256 + 128 * ch, 384 + 128 * ch), a("lhb", 256 + 128 * ch, 384 + 128 * ch), a("idb"))
+        boost[0] = 0.0
         if not last:
-            act(a("rcb"), a("pr", 0, 256), AF.Copy)
-            for ch in H:
-                mm(a("pl", 48 + 8 * ch, 56 + 8 * ch), a("rcb", 128 * ch, 128 * ch + 128), a("k0"))
             next_saved()
+        boost[0] = UQ
         tt(a("eqm"), a("mk2"), a("pr", 256, 512), OP.is_gt)
         if last:
             break
         tt(mkA, keep, a("eqm"), OP.add)
-        cp(a("pai"), a("pl", 48, 64))
-        ts(a("paj"), a("pai"), 1, OP.bitwise_and)
-        tt(a("lim"), a("eight"), a("paj"), OP.subtract)
+        boost[0] = 0.0
 
+    boost[0] = 0.0
     ts(a("op"), a("oi"), 10, OP.arith_shift_right, 4095, OP.bitwise_and)
     ts(mkA, a("op"), -512, OP.mult, -16 - U, OP.add)
     tt(a("oy"), a("oi"), mkA, OP.add)
@@ -412,19 +424,20 @@ def rank_program(g, core, T, topo):
     lg, n = {}, len(prog)
     dep, succ = [[] for _ in range(n)], [[] for _ in range(n)]
     for i, p in enumerate(prog):
-        ds = {}
-        for e, kind in meets(p["q"] if p["kind"] == "c" else "#%d" % i, p["acc"], lg):
+        ds, q = {}, p["q"] if p["kind"] == "c" else "#%d" % i
+        for e, kind in meets(q, p["acc"], lg):
             ds[e[3]] = 0.0 if (p["q"] == "t" and prog[e[3]]["q"] == "t") else WAKE
         if p["kind"] == "n":
             ds[p["extra"][2]] = 0.0
-        note(p["q"] if p["kind"] == "c" else "#%d" % i, p["acc"], lg, i)
+        note(q, p["acc"], lg, i)
         dep[i] = sorted(ds.items())
         for d, w in dep[i]:
             succ[d].append((i, w))
-    rankp = [0.0] * n
+    rankp, base = [0.0] * n, [0.0] * n
     for i in range(n - 1, -1, -1):
         p = prog[i]
-        rankp[i] = p["dur"] + p["lat"] + max([w + rankp[j] for j, w in succ[i]] + [0.0])
+        base[i] = p["dur"] + p["lat"] + max([w + base[j] for j, w in succ[i]] + [0.0])
+        rankp[i] = base[i] + p["up"]
     free = {q: 0.0 for q in list(Q) + ["net"]}
     left = [len(d) for d in dep]
     done = [0.0] * n
@@ -439,8 +452,14 @@ def rank_program(g, core, T, topo):
             if not ready[q]:
                 continue
             t0 = max(free[q], min(e for e, i in ready[q])) if q != "net" else min(e for e, i in ready[q])
-            c = max(((rankp[i], -i) for e, i in ready[q] if e <= t0 + 1e-9))
+            c = max((rankp[i], -i, e) for e, i in ready[q] if e <= t0 + SLACK)
             i = -c[1]
+            if c[2] > t0:
+                short = [(rankp[k], -k) for e, k in ready[q] if e <= t0 + 1e-9 and t0 + prog[k]["dur"] <= c[2] + OVER]
+                if short:
+                    i = -max(short)[1]
+                else:
+                    t0 = c[2]
             if best is None or t0 < best[0]:
                 best = (t0, i, q)
         t0, i, q = best

@@ -31,9 +31,12 @@ PSUM = [n for n in SCRATCH if SCRATCH[n][0] == "psum"]
 GCH = [(0, 1024), (1024, 2048), (2048, 3072), (3072, 4096)]
 VCH = [(0, 1024), (1024, 2048), (2048, 3072), (3072, 3584), (3584, 4096)]
 PH = [(0, 128), (128, 256)]
-KS = (0, 2, 4)
+SKW = 512
+KS = (1, 3, 5)
 CYC, CG, FIX, GFIX, SFIX, WAKE, PEC = 0.00083, 1.5, 0.01, 0.05, 0.06, 0.11, 0.00071
 SLACK, OVER, UP, UQ = 0.1, 0.05, 1.5, 3.0
+PREF = {33: 8, 55: -8, 110: 8, 124: -3, 125: -8, 137: 8, 142: -1.5, 146: 1.5, 166: -3, 211: -8, 214: -8, 224: 3,
+        511: -1.5, 512: -3, 527: -3, 581: -3, 605: 3, 622: -3}
 
 
 def rank_program(g, core, T, topo):
@@ -44,7 +47,7 @@ def rank_program(g, core, T, topo):
     SEM = {"v": "sv", "s": "ss", "t": "st", "g": "sg"}
     know = {q: {} for q in Q}
     cnt, snap, nd = {}, {}, [0]
-    prog, boost = [], [0.0]
+    prog, boost, mark = [], [0.0], [0]
 
     def a(n, lo=0, hi=None, st=1, r=None, r0=0):
         if n in VIEW:
@@ -92,7 +95,7 @@ def rank_program(g, core, T, topo):
             lg[n] = old + [(lo, hi, kind, ref, q)]
 
     def add(q, call, reads, writes, dur, lat=0.0, kind="c", extra=None):
-        prog.append({"up": boost[0], "q": q, "call": call, "acc": flat(reads, writes), "dur": dur, "lat": lat, "kind": kind, "extra": extra})
+        prog.append({"up": boost[0], "id": len(prog) - mark[0], "q": q, "call": call, "acc": flat(reads, writes), "dur": dur, "lat": lat, "kind": kind, "extra": extra})
 
     def vcost(o, ins, two=False):
         n = max(size(x) for x in ins)
@@ -151,17 +154,16 @@ def rank_program(g, core, T, topo):
         add("g", call, [src], [], 0.6, 0.0, "r", (rsem, len(topo.engines(core, to))))
         add("net", None, [], [dst], 0.0, 2.2 + 0.3 * size(dst) / 256, "n", (rsem, len(topo.engines(core, to)), len(prog) - 1))
 
-    dma("y", a("ini", 0, 256), dr(T.gs[:]))
-    dma("s", a("ini", 256, 512), dr(T.gf[:]))
-    dma("y", a("ini", 512, 768), dr(T.gcl[:]))
-    dma("s", a("fri"), dr(T.fr[:]))
-    NS = 4
-    for j in range(NS):
-        w = 4096 // NS
-        dma("ys"[j % 2], a("ski", w * j, w * j + w), dr(T.sk[:, w * j:w * j + w]), 3.0 + 1.5 * j)
-    dma("s", a("xr", 592, 4096), dr(T.x[:, 0:3504]), 11.0)
-    dma("y", a("xr", 0, 592), dr(T.x[:, 3504:4096]), 11.0)
-    dma("y", a("thi", 0, 1), dr(T.th[:]), 11.0)
+    boost[0] = 1000.0
+    LD = [("ini", 0, 256, T.gs[:], 0.01), ("ini", 256, 512, T.gf[:], 0.01), ("ini", 512, 768, T.gcl[:], 0.01), ("fri", 0, 256, T.fr[:], 0.15)]
+    LD += [("ski", w, w + SKW, T.sk[:, w:w + SKW], 0.6 * SKW / 512) for w in range(0, 4096, SKW)]
+    LD += [("thi", 0, 1, T.th[:], 0.01), ("xr", 592, 4096, T.x[:, 0:3504], 2.3), ("xr", 0, 592, T.x[:, 3504:4096], 0.4)]
+    came = 0.0
+    for j, (n, lo, hi, src, us) in enumerate(LD):
+        boost[0] -= 10.0
+        came += us
+        dma("ys"[j % 2], a(n, lo, hi), dr(src), 2.0 + came - 0.05 * j)
+    boost[0] = 0.0
     iota(a("ci"), [[1, 256]], 0, 0)
     iota(a("pi"), [[0, 256]], 0, 1)
     iota(a("il"), [[128, 2], [0, 8]], 16, 1)
@@ -295,6 +297,7 @@ def rank_program(g, core, T, topo):
     for t in range(RO):
         F, last = "f%d" % t, t == RO - 1
         b = 32 * ((t + 4) % 5)
+        mark[0] = len(prog) - 500 if t else mark[0]
         if t == 0:
             clause_side(4)
         if t == 0:
@@ -437,7 +440,7 @@ def rank_program(g, core, T, topo):
     for i in range(n - 1, -1, -1):
         p = prog[i]
         base[i] = p["dur"] + p["lat"] + max([w + base[j] for j, w in succ[i]] + [0.0])
-        rankp[i] = base[i] + p["up"]
+        rankp[i] = base[i] + p["up"] + PREF.get(p["id"], 0.0)
     free = {q: 0.0 for q in list(Q) + ["net"]}
     left = [len(d) for d in dep]
     done = [0.0] * n

from concourse.mybir import AluOpType, ActivationFunctionType

OP = AluOpType
AF = ActivationFunctionType
U = 1 << 22
NF, RO, N = 256, 5, 4
H = (0, 1)
F32, BF, I32, U16 = "float32", "bfloat16", "int32", "uint16"
SCRATCH = {}


def _bufs(where, dtype, text):
    for w in text.split():
        n, c = w.split(":")
        r, c = (c.split("x") if "x" in c else (128, c))
        SCRATCH[n] = (where, [int(r), int(c)], dtype)


_bufs("sbuf", F32, "skv:4096 skt:4096 inf:8x512 ine:8x512 thf:8 tabb:768 tabh:768 j8:8 mske:256 rst:256 idf:128 onef:128 thrt:256 "
      "iw:16 il:16 lim:16 fb:256 hb:256 tg:256 tc:256 f3p:256 own3:256 x3:256 eqm:256 nov:256 key:256 cnt:256 sm:256 "
      "cl:16 smx:16 pgc:512 thp:256 clst:32 lsb:32 lh:512 we:16 wf:16 wh:16 sc:32 sv:32 s1:32 s2:32 t1:16 st:16 par:64 "
      "fot:64x128 oy:256 oy2:256 oz:256 f0:768 f1:768 f2:768 f3:768 f4:768 snd0:256 snd1:256 snd2:256 snd3:256")
_bufs("sbuf", BF, "idk:128 xr:4096 ub:4096 hi:256 em:256 df:4096 ab:4096 b16:8 idb:128 k0:8 zero:16 rcb:256 oneb:128 krow:128 fr5:256 mk2:256 sel:256 lhb:512")
_bufs("sbuf", I32, "ski:4096 ini:8x768 fri:256 thi:8 thj:8 pi:256 ci:256 pm:256 cm:256 ps:8 rawg:256 rawc:256 ga:256 ca:256 "
      "pg:256 qg:256 prg:256 rg:256 pc:256 qc:256 prc:256 rc:256 wi:32 wq:32 s3:32 t4:16 t5:16 t6:16 t7:16 t8:16 fip:64 oi:256 op:256")
_bufs("sbuf", U16, "ug:256 uc:256 el:16 fl:16 hl:16 sl:160 sarr:80")
_bufs("psum", F32, "b0:512 b1:512 pe:512 pl:512 pr:512 sr:512 d0:512 d1:512")
SEMAPHORES = ["sv", "ss", "st", "sg", "rl"] + ["as%d" % t for t in range(4)] + ["ac%d" % t for t in range(4)] + ["d%d" % t for t in range(24)]
VIEW = {"sks": ("df", 0, 4096), "frs": ("op", 0, 256), "frm": ("oy", 0, 256), "dg": ("oz", 0, 128), "fin": ("lh", 0, 64), "fiq": ("lh", 64, 64), "fim": ("lh", 128, 64)}
PSUM = [n for n in SCRATCH if SCRATCH[n][0] == "psum"]
GCH = [(0, 1024), (1024, 2048), (2048, 3072), (3072, 4096)]
VCH = [(0, 1024), (1024, 2048), (2048, 3072), (3072, 3584), (3584, 4096)]
PH = [(0, 128), (128, 256)]
SKW = 512
KS = (1, 3, 5)
CYC, CG, FIX, GFIX, SFIX, WAKE, PEC = 0.00083, 1.5, 0.01, 0.05, 0.06, 0.11, 0.00071
SLACK, OVER, UP, UQ = 0.1, 0.05, 1.5, 3.0
PREF = {33: 8, 55: -8, 110: 8, 124: -3, 125: -8, 137: 8, 142: -1.5, 146: 1.5, 166: -3, 211: -8, 214: -8, 224: 3,
        511: -1.5, 512: -3, 527: -3, 581: -3, 605: 3, 622: -3}


def rank_program(g, core, T, topo):
    rank = T.rank_of(core)
    if rank is None:
        return
    Q = {"v": g.vector, "s": g.scalar, "t": g.tensor, "g": g, "y": g.sync}
    SEM = {"v": "sv", "s": "ss", "t": "st", "g": "sg"}
    know = {q: {} for q in Q}
    cnt, snap, nd = {}, {}, [0]
    prog, boost, mark = [], [0.0], [0]

    def a(n, lo=0, hi=None, st=1, r=None, r0=0):
        if n in VIEW:
            b, c, w = VIEW[n]
            return a(b, c + lo, c + (w if hi is None else hi), st, r, r0)
        return (n, lo, SCRATCH[n][1][1] if hi is None else hi, st, r0, SCRATCH[n][1][0] if r is None else r)

    def ind(w, o):
        return ("@", w, o)

    def ap(o):
        if o[0] == "@":
            return ap(o[1]).indirect(ap(o[2]))
        if o[0] == "!":
            return o[1]
        b = T[o[0]]
        return b[o[4]:o[5], o[1]:o[2]] if o[3] == 1 else b[o[4]:o[5], o[1]:o[2]:o[3]]

    def parts(o):
        return [o[1], o[2]] if o[0] == "@" else [] if o[0] == "!" else [o]

    def flat(reads, writes):
        return [(k, p) for k, ops in (("r", reads), ("w", writes)) for o in ops for p in parts(o)]

    def size(o):
        return (o[2][2] - o[2][1]) * 16 if o[0] == "@" else (o[2] - o[1] + o[3] - 1) // o[3]

    def meets(q, acc, lg):
        for kind, (n, lo, hi, st, r0, r1) in acc:
            for e in lg.get(n, []):
                if n in PSUM and e[4] != q:
                    yield e, kind
                elif lo < e[1] and e[0] < hi and "w" in (kind, e[2]):
                    yield e, kind
                elif n in PSUM and q == "t" and kind == "w" and e[2] == "w":
                    yield e, kind

    def note(q, acc, lg, ref):
        for kind, (n, lo, hi, st, r0, r1) in acc:
            old = lg.get(n, [])
            if kind == "w" and st == 1 and n not in PSUM:
                old = [e for e in old if not (lo <= e[0] and e[1] <= hi)]
            if n in PSUM and kind == "w":
                old = [e for e in old if e[4] == q and not (st == 1 and lo <= e[0] and e[1] <= hi)]
            lg[n] = old + [(lo, hi, kind, ref, q)]

    def add(q, call, reads, writes, dur, lat=0.0, kind="c", extra=None):
        prog.append({"up": boost[0], "id": len(prog) - mark[0], "q": q, "call": call, "acc": flat(reads, writes), "dur": dur, "lat": lat, "kind": kind, "extra": extra})

    def vcost(o, ins, two=False):
        n = max(size(x) for x in ins)
        if any(x[0] == "@" for x in ins):
            return GFIX + CYC * CG * n
        f = 2.0 if two and not any(x[0] in PSUM for x in ins) else 1.0
        return FIX + CYC * max(64, n * f)

    def tt(o, x, y, op):
        add("v", lambda: g.vector.tensor_tensor(ap(o), ap(x), ap(y), op), [x, y], [o], vcost(o, [x, y], True))

    def ts(o, x, s1, op0, s2=None, op1=None):
        def call():
            if op1 is None:
                return g.vector.tensor_scalar(ap(o), ap(x), s1, None, op0)
            return g.vector.tensor_scalar(ap(o), ap(x), s1, s2, op0, op1)
        add("v", call, [x], [o], vcost(o, [x]))

    def cp(o, x):
        add("v", lambda: g.vector.tensor_copy(ap(o), ap(x)), [x], [o], vcost(o, [x]))

    def scan(o, d0, d1, op0, op1):
        add("v", lambda: g.vector.tensor_tensor_scan(ap(o), ap(d0), ap(d1), 0.0, op0, op1), [d0, d1], [o], vcost(o, [d1]))

    def act(o, x, func, scale=1.0, bias=0.0):
        rd = [x] + ([scale] if isinstance(scale, tuple) else [])

        def call():
            return g.scalar.activation(ap(o), ap(x), func, bias, ap(scale) if isinstance(scale, tuple) else scale)
        add("s", call, rd, [o], SFIX + CYC * size(x) * (CG if x[0] == "@" else 1.0))

    def mm(o, l, r, start=True, stop=True):
        w = 4 if SCRATCH[l[0]][2] == F32 else 1
        add("t", lambda: g.tensor.matmul(ap(o), ap(l), ap(r), start, stop), [l, r], [o], 0.03 + PEC * w * max(min(64, size(l)), size(r)))

    def tr(o, x, i):
        add("t", lambda: g.tensor.transpose(ap(o), ap(x), ap(i)), [x, i], [o], 0.3)

    def iota(o, pat, base, cmul):
        def call():
            if SCRATCH[o[0]][2] == I32:
                return g.iota(ap(o), pat, base, cmul)
            return g.iota(ap(o), pat, base, cmul, allow_small_or_imprecise_dtypes=True)
        add("g", call, [], [o], 0.15 + 2 * CYC * size(o))

    def dma(q, out, in_, lat=2.0):
        add(q, lambda: Q[q].dma_start(ap(out), ap(in_)), [in_], [out], 0.1, lat, "d")

    def dr(x):
        return ("!", x)

    def send(dst, src, to, rsem):
        def call():
            rid, pid, _ = topo.addr(to)
            g.remote_dma(ap(dst), ap(src), T.sem[rsem], T.sem["rl"], pid, rid, topo.mask(core, to))
        add("g", call, [src], [], 0.6, 0.0, "r", (rsem, len(topo.engines(core, to))))
        add("net", None, [], [dst], 0.0, 2.2 + 0.3 * size(dst) / 256, "n", (rsem, len(topo.engines(core, to)), len(prog) - 1))

    boost[0] = 1000.0
    LD = [("ini", 0, 256, T.gs[:], 0.01), ("ini", 256, 512, T.gf[:], 0.01), ("ini", 512, 768, T.gcl[:], 0.01), ("fri", 0, 256, T.fr[:], 0.15)]
    LD += [("ski", w, w + SKW, T.sk[:, w:w + SKW], 0.6 * SKW / 512) for w in range(0, 4096, SKW)]
    LD += [("thi", 0, 1, T.th[:], 0.01), ("xr", 592, 4096, T.x[:, 0:3504], 2.3), ("xr", 0, 592, T.x[:, 3504:4096], 0.4)]
    came = 0.0
    for j, (n, lo, hi, src, us) in enumerate(LD):
        boost[0] -= 10.0
        came += us
        dma("ys"[j % 2], a(n, lo, hi), dr(src), 2.0 + came - 0.05 * j)
    boost[0] = 0.0
    iota(a("ci"), [[1, 256]], 0, 0)
    iota(a("pi"), [[0, 256]], 0, 1)
    iota(a("il"), [[128, 2], [0, 8]], 16, 1)
    iota(a("tabb", 0, 512), [[1, 512]], 16, 0)
    iota(a("tabb", 512, 768), [[1, 256]], 16, 0)
    iota(a("cm"), [[0, 16], [1, 16]], 0, 0)
    iota(a("tabh", 0, 512), [[0, 512]], 0, 0)
    iota(a("tabh", 512, 768), [[0, 256]], 1, 0)
    iota(a("onef"), [[0, 128]], 1, 0)
    iota(a("oneb"), [[0, 128]], 1, 0)
    iota(a("zero"), [[0, 16]], 0, 0)
    iota(a("lim"), [[0, 16]], 8, 0)
    iota(a("krow", 0, 128, 1, 1), [[0, 8], [-1, 16]], 16, 0)
    tt(a("idf"), a("pi", 0, 128), a("ci", 0, 128), OP.is_equal)
    act(a("idb"), a("idf"), AF.Copy)
    act(a("idk"), a("idf"), AF.Copy, 8192.0)
    ts(a("ps"), a("pi", 0, 8), 4, OP.arith_shift_right)
    tt(a("j8"), a("ps"), a("ci", 0, 8), OP.is_equal)
    ts(a("pm"), a("pi"), 15, OP.bitwise_and)
    tt(a("mske"), a("pm"), a("cm"), OP.is_equal)
    cp(a("el"), a("ci", 0, 16))
    ts(a("inf", 0, 256), a("ini", 0, 256), 1024, OP.mult, 16, OP.add)
    ts(a("inf", 256, 512), a("ini", 512, 768), 1024, OP.mult, 16, OP.add)
    tt(a("ine", 0, 256), a("inf", 0, 256), a("ini", 256, 512), OP.add)
    tt(a("ine", 256, 512), a("inf", 256, 512), a("ci", 0, 256, 1, 8), OP.add)
    for x in H:
        for ch in H:
            mm(a("pl", 16 * x + 8 * ch, 16 * x + 8 * ch + 8), a("ine", 256 * x + 128 * ch, 256 * x + 128 * ch + 128), a("idf", 0, 8, 1, 8))
    cp(a("lsb"), a("pl", 0, 32))
    mkA, keep, emhi = a("b1", 0, 256), a("b1", 256, 512), a("pe", 256, 512)
    pw = (a("pl", 64, 80), a("pl", 80, 96))

    def to_w(x):
        tt(a("lh", 256 * x, 256 * x + 256), ind(a("lsb", 16 * x, 16 * x + 16), a("el")), a("mske"), OP.mult)
        for ch in H:
            mm(a("pl", 64 + 16 * x + 8 * ch, 72 + 16 * x + 8 * ch), a("lh", 256 * x + 128 * ch, 256 * x + 128 * ch + 128), a("j8"))

    def upper(o, x):
        ts(o, x, 1.0 / 1024, OP.mult, -1.0 / 64, OP.add)

    def goal_lists(t):
        ts(a("wi", 0, 16), pw[0], -16, OP.add)
        ts(a("wq", 0, 16), a("wi", 0, 16), 1023, OP.bitwise_and)
        cp(a("fl"), a("wq", 0, 16))
        upper(a("sl", 32 * t, 32 * t + 16), pw[0])

    def clause_lists(t):
        upper(a("sl", 32 * t + 16, 32 * t + 32), pw[1])
        ts(a("wi", 16, 32), pw[1], -16, OP.add)
        ts(a("wq", 16, 32), a("wi", 16, 32), 1023, OP.bitwise_and)
        tt(a("we"), a("wq", 16, 32), a("iw"), OP.is_equal)
        ts(a("wf"), a("we"), 512, OP.mult)
        tt(a("wh"), a("wf"), a("wq", 16, 32), OP.add)
        cp(a("hl"), a("wh"))
        act(a("hi"), ind(a("tabh"), a("hl")), AF.Identity)
        act(a("hb"), ind(a("tabb"), a("hl")), AF.Identity)

    def clause_side(t):
        tt(a("tc"), ind(a("skt"), a("sl", 32 * t + 16, 32 * t + 32)), a("hb"), OP.add)
        mm(a("d1", 256, 512), a("idb"), a("hi"), True, False)
        mm(a("d1", 256, 512), a("idb"), a("em"), False, True)
        act(emhi, a("d1", 256, 512), AF.Relu, 1.0, -1.0)

    def next_saved():
        upper(a("s3"), a("sv"))
        tt(a("t4"), a("s3", 0, 16), a("s3", 16, 32), OP.mult)
        ts(a("t8"), a("s3", 16, 32), 1, OP.add)
        ts(a("t5"), a("t4"), 5, OP.arith_shift_right)
        tt(a("t6"), a("t5"), a("t8"), OP.add)
        ts(a("t7"), a("t6"), 4095, OP.bitwise_and)
        ts(a("t1"), a("t7"), 1024, OP.mult)
        tt(a("st"), a("t1"), a("il"), OP.add)

    def own_parts(F):
        act(a("em"), a(F, 0, 256), AF.Relu, -1.0, 1.0)
        act(a("f3p"), a(F, 0, 256), AF.Relu, 1.0, -float(U))
        act(a("own3"), a("f3p"), AF.Identity, 1.0, float(U))

    ts(a("wf"), a("ci", 0, 16), 16, OP.mult)
    tt(a("iw"), a("wf"), a("pm", 0, 16), OP.add)
    to_w(0)
    goal_lists(4)
    to_w(1)
    clause_lists(4)
    act(a("fb"), ind(a("tabb", 0, 512), a("fl")), AF.Identity)
    ts(a("frs"), a("fri"), 9, OP.arith_shift_right)
    ts(keep, a("frs"), 512, OP.mult, 16 + U, OP.add)
    tt(a("x3"), a("fri"), keep, OP.add)
    ts(a("frm"), a("fri"), 0, OP.is_ge)
    tt(a("f0", 0, 256), a("x3"), a("frm"), OP.mult)
    ts(mkA, a("frm"), 2, OP.mult)
    act(a("f0", 256, 512), a("f0", 0, 256), AF.Identity)
    own_parts("f0")
    for j in range(8):
        s = 512 * j
        if j in KS:
            h = a(("pr", "sr")[j % 2])
            cp(a("skv", s, s + 512), a("ski", s, s + 512))
            act(a("sks", s, s + 512), a("skv", s, s + 512), AF.Sign, -1.0, 4095.5)
            mm(h, a("idf"), a("skv", s, s + 512), True, False)
            mm(h, a("idk"), a("sks", s, s + 512), False, True)
            act(a("skt", s, s + 512), h, AF.Identity, 1024.0, float(U))
            continue
        h = a(("d0", "d1")[j % 2])
        ts(h, a("ski", s, s + 512), 4096, OP.is_lt, 16384, OP.mult)
        tt(a("skv", s, s + 512), a("ski", s, s + 512), h, OP.add)
        act(a("skt", s, s + 512), a("skv", s, s + 512), AF.Identity, 1024.0, -float(U))
    act(a("b16"), a("j8"), AF.Copy, 16.0)
    ts(a("k0"), a("pm", 0, 8), 0, OP.is_equal)
    ts(a("rst"), a("cm"), 0, OP.not_equal)
    ts(a("thf", 0, 1), a("thi", 0, 1), 16, OP.mult, 16, OP.add)
    act(a("dg"), a("idf"), AF.Copy, a("thf", 0, 1))
    mm(a("pr", 0, 128), a("onef"), a("dg"))
    for ch in H:
        act(a("thrt", 128 * ch, 128 * ch + 128), a("pr", 0, 128), AF.Copy)
    ts(a("thj", 0, 1), a("thi", 0, 1), -1, OP.add)
    ts(a("thj", 1, 2), a("thj", 0, 1), 1, OP.arith_shift_right)
    ts(a("thf", 1, 2), a("thj", 1, 2), 16, OP.mult, 16, OP.add)
    act(a("sv"), a("lsb"), AF.Copy)
    next_saved()

    def places(raw, m, p, q, pr, r, u):
        for w in PH:
            ts(a(m, *w), a(raw, *w), U - 1, OP.bitwise_and)
            ts(a(q, *w), a(raw, *w), 1023, OP.bitwise_and)
            ts(a(p, *w), a(m, *w), 1.0 / 1024, OP.mult, 592 - 1.0 / 64, OP.add)
            tt(a(pr, *w), a(p, *w), a(q, *w), OP.mult)
            ts(a(r, *w), a(pr, *w), 4, OP.arith_shift_right, 4095, OP.bitwise_and)
            cp(a(u, *w), a(r, *w))

    for t in range(RO):
        F, last = "f%d" % t, t == RO - 1
        b = 32 * ((t + 4) % 5)
        mark[0] = len(prog) - 500 if t else mark[0]
        if t == 0:
            clause_side(4)
        if t == 0:
            tt(a("tg"), ind(a("skt"), a("sl", b, b + 16)), a("fb"), OP.add)
            tt(a("rawg"), ind(a(F, 0, 512), a("fl")), a("tg"), OP.max)
        else:
            tt(a("tg"), ind(a("skt"), a("sarr", 16 * t, 16 * t + 16)), a("tabb", 256, 512), OP.add)
            for lo, hi in PH:
                tt(a("rawg", lo, hi), a(F, 256 + lo, 256 + hi), a("tg", lo, hi), OP.max)
        boost[0] = UP
        places("rawg", "ga", "pg", "qg", "prg", "rg", "ug")
        boost[0] = 0.0
        for lo, hi in GCH:
            act(a("ub", lo, hi), ind(a("xr"), a("ug", lo // 16, hi // 16)), AF.Identity)
        for lo, hi in PH:
            e = a("b0", lo, hi)
            tt(e, a("pe", 256 + lo, 256 + hi), a("ga", lo, hi), OP.mult)
            tt(a(F, 512 + lo, 512 + hi), a("own3", lo, hi), e, OP.add)
        tt(a("rawc"), ind(a(F), a("hl")), a("tc"), OP.max)
        places("rawc", "ca", "pc", "qc", "prc", "rc", "uc")
        for lo, hi in VCH:
            tt(a("df", lo, hi), ind(a("xr"), a("uc", lo // 16, hi // 16)), a("ub", lo, hi), OP.subtract)
            act(a("ab", lo, hi), a("df", lo, hi), AF.Abs)
        for ch in H:
            D = ("d0", "d1")[ch]
            mm(a(D, 0, 128), a("oneb", 0, 128, 1, 1), a("krow", 0, 128, 1, 1), True, False)
            for k in range(16):
                mm(a(D, k, 128, 16), a("ab", 2048 * ch + k, 2048 * ch + 2048, 16), a("b16"), False, k == 15)
        mm(a("pr", 256, 512), a("idf"), a(F, 512, 768))
        tt(a("fr5"), a("rawc"), a("pr", 256, 512), OP.is_equal)
        tt(a("mk2"), a("fr5"), mkA, OP.max)
        for ch in H:
            D, R = a(("d0", "d1")[ch], 0, 128), a(("sr", "pe")[ch], 0, 128)
            lo, hi, l8 = 128 * ch, 128 * ch + 128, (8 * ch, 8 * ch + 8)
            tt(a("nov", lo, hi), D, a("thrt", lo, hi), OP.is_le)
            tt(a("key", lo, hi), a("nov", lo, hi), D, OP.mult)
            scan(a("cnt", lo, hi), a("rst", lo, hi), a("nov", lo, hi), OP.mult, OP.add)
            scan(a("sm", lo, hi), a("rst", lo, hi), a("key", lo, hi), OP.mult, OP.max)
            tt(a("cl", *l8), a("cnt", lo + 15, hi, 16), a("lim", *l8), OP.is_le)
            tt(a("smx", *l8), a("sm", lo + 15, hi, 16), a("cl", *l8), OP.add)
            tt(a("sel", lo, hi), ind(a("smx", *l8), a("el", 0, 8)), a("key", lo, hi), OP.is_equal)
            mm(R, a("sel", lo, hi), a("idb"))
            tt(a("pgc", lo, hi), a("ga", lo, hi), R, OP.mult)
            tt(a("pgc", 256 + lo, 256 + hi), a("ca", lo, hi), R, OP.mult)
        act(a("lhb", 0, 256), ind(a("cl"), a("el")), AF.Identity)
        for ch in H:
            mm(a("pr", 128 * ch, 128 * ch + 128), a("lhb", 128 * ch, 128 * ch + 128), a("idb"))
        tt(keep, a("mk2"), a("pr", 0, 256), OP.is_gt)
        tt(a("oi") if last else a(F, 0, 256), a(F, 512, 768), keep, OP.mult)
        if not last:
            act(a("rcb"), a("pr", 0, 256), AF.Copy)
        for ch in H:
            act(a("thp", 128 * ch, 128 * ch + 128), a(("sr", "pe")[ch], 0, 128), AF.Copy, a("thf", 1, 2))
        tt(a("clst", 0, 16), a("cl"), a("sv", 0, 16), OP.mult)
        tt(a("clst", 16, 32), a("cl"), a("st"), OP.mult)
        for x in H:
            B, c = (("pl", 0), ("d1", 128))[x]
            mm(a(B, c, c + 16), a("idb"), a("zero"), True, False)
            mm(a(B, c, c + 8), a("pgc", 256 * x, 256 * x + 128), a("j8"), False, False)
            mm(a(B, c, c + 16), a("idf"), a("clst", 16 * x, 16 * x + 16), False, False)
            mm(a(B, c + 8, c + 16), a("pgc", 256 * x + 128, 256 * x + 256), a("j8"), False, True)
            cp(a("lsb", 16 * x, 16 * x + 16), a(B, c, c + 16))
        if not last:
            to = T.cores[(rank + 1 + t % 3) % N]
            to_w(0)
            goal_lists(t)
            send(a("sarr", 16 * t + 16, 16 * t + 32), a("sl", 32 * t, 32 * t + 16), to, "as%d" % t)
            act(a("snd%d" % t), ind(a(F, 0, 512), a("fl")), AF.Identity)
            send(a("f%d" % (t + 1), 256, 512), a("snd%d" % t), to, "ac%d" % t)
            to_w(1)
        for ch in H:
            mm(a("pl", 32 + 8 * ch, 40 + 8 * ch), a("thp", 128 * ch, 128 * ch + 128), a("j8"))
        if not last:
            for ch in H:
                mm(a("pl", 48 + 8 * ch, 56 + 8 * ch), a("rcb", 128 * ch, 128 * ch + 128), a("k0"))
        tt(a("sc", 0, 16), a("smx"), a("pl", 32, 48), OP.is_le)
        if not last:
            clause_lists(t)
            act(a("par", 0, 16), a("pl", 48, 64), AF.Abs, 1.0, -4.0)
            act(a("par", 16, 32), a("par", 0, 16), AF.Abs, 1.0, -2.0)
            act(a("par", 32, 48), a("par", 16, 32), AF.Abs, 1.0, -1.0)
            act(a("lim"), a("par", 32, 48), AF.Identity, 1.0, 7.0)
            own_parts(F)
            act(a("f%d" % (t + 1), 0, 256), a(F, 0, 256), AF.Identity)
            clause_side(t)
        boost[0] = UQ
        act(a("lhb", 256, 512), ind(a("sc", 0, 16), a("el")), AF.Identity, -1.0, 1.0)
        boost[0] = 0.0
        tt(a("s1"), a("lsb"), a("sv"), OP.subtract)
        tt(a("sc", 16, 32), a("sc", 0, 16), a("cl"), OP.add)
        tt(a("s2"), a("s1"), a("sc"), OP.mult)
        tt(a("sv"), a("sv"), a("s2"), OP.add)
        boost[0] = UQ
        for ch in H:
            mm(a("pr", 256 + 128 * ch, 384 + 128 * ch), a("lhb", 256 + 128 * ch, 384 + 128 * ch), a("idb"))
        boost[0] = 0.0
        if not last:
            next_saved()
        boost[0] = UQ
        tt(a("eqm"), a("mk2"), a("pr", 256, 512), OP.is_gt)
        if last:
            break
        tt(mkA, keep, a("eqm"), OP.add)
        boost[0] = 0.0

    boost[0] = 0.0
    ts(a("op"), a("oi"), 10, OP.arith_shift_right, 4095, OP.bitwise_and)
    ts(mkA, a("op"), -512, OP.mult, -16 - U, OP.add)
    tt(a("oy"), a("oi"), mkA, OP.add)
    tt(a("oy2"), keep, a("eqm"), OP.subtract)
    ts(mkA, a("oy"), 2, OP.mult, -1, OP.max)
    tt(a("oz"), a("oy2"), mkA, OP.add)
    dma("y", dr(T.yf[:]), a("oz"))
    cp(a("fin", 0, 32), a("lsb"))
    cp(a("fin", 32, 64), a("sv"))
    upper(a("fip"), a("fin"))
    ts(a("fiq", 0, 48), a("fip", 0, 48), -512, OP.mult, -16, OP.add)
    tt(a("fim", 0, 48), a("fin", 0, 48), a("fiq", 0, 48), OP.add)
    cp(a("fim", 48, 64), a("fip", 48, 64))
    tr(a("pl", 0, 128, 1, 64), a("fim"), a("idf"))
    cp(a("fot"), a("pl", 0, 128, 1, 64))
    for j, y in enumerate((T.yg, T.yc, T.ysg, T.yk)):
        for ch in H:
            r0 = 16 * j + 8 * ch
            dma("ys"[(2 * j + ch) % 2], dr(y[:, 128 * ch:128 * ch + 128]), a("fot", 0, 128, 1, r0 + 8, r0))

    lg, n = {}, len(prog)
    dep, succ = [[] for _ in range(n)], [[] for _ in range(n)]
    for i, p in enumerate(prog):
        ds, q = {}, p["q"] if p["kind"] == "c" else "#%d" % i
        for e, kind in meets(q, p["acc"], lg):
            ds[e[3]] = 0.0 if (p["q"] == "t" and prog[e[3]]["q"] == "t") else WAKE
        if p["kind"] == "n":
            ds[p["extra"][2]] = 0.0
        note(q, p["acc"], lg, i)
        dep[i] = sorted(ds.items())
        for d, w in dep[i]:
            succ[d].append((i, w))
    rankp, base = [0.0] * n, [0.0] * n
    for i in range(n - 1, -1, -1):
        p = prog[i]
        base[i] = p["dur"] + p["lat"] + max([w + base[j] for j, w in succ[i]] + [0.0])
        rankp[i] = base[i] + p["up"] + PREF.get(p["id"], 0.0)
    free = {q: 0.0 for q in list(Q) + ["net"]}
    left = [len(d) for d in dep]
    done = [0.0] * n
    ready = {q: [] for q in free}
    for i in range(n):
        if not left[i]:
            ready[prog[i]["q"]].append((0.0, i))
    plan = []
    for _ in range(n):
        best = None
        for q in free:
            if not ready[q]:
                continue
            t0 = max(free[q], min(e for e, i in ready[q])) if q != "net" else min(e for e, i in ready[q])
            c = max((rankp[i], -i, e) for e, i in ready[q] if e <= t0 + SLACK)
            i = -c[1]
            if c[2] > t0:
                short = [(rankp[k], -k) for e, k in ready[q] if e <= t0 + 1e-9 and t0 + prog[k]["dur"] <= c[2] + OVER]
                if short:
                    i = -max(short)[1]
                else:
                    t0 = c[2]
            if best is None or t0 < best[0]:
                best = (t0, i, q)
        t0, i, q = best
        ready[q] = [x for x in ready[q] if x[1] != i]
        if q != "net":
            free[q] = t0 + prog[i]["dur"]
        done[i] = t0 + prog[i]["dur"] + prog[i]["lat"]
        plan.append(i)
        for j, w in succ[i]:
            left[j] -= 1
            if not left[j]:
                ready[prog[j]["q"]].append((max(done[d] + w2 for d, w2 in dep[j]), j))

    def wait(q, sem, c):
        if know[q].get(sem, 0) < c:
            Q[q].wait_ge(T.sem[sem], c)
            for k, v in snap.get((sem, c), {}).items():
                know[q][k] = max(know[q].get(k, 0), v)
            know[q][sem] = c

    ref = {}
    for i in plan:
        p = prog[i]
        q = p["q"]
        if p["kind"] != "n":
            want = {}
            for d, w in dep[i]:
                if q == "t" and prog[d]["q"] == "t":
                    continue
                sem, c = ref[d]
                want[sem] = max(want.get(sem, 0), c)
            for sem in sorted(want, key=lambda s: (s == SEM.get(q), s)):
                wait(q, sem, want[sem])
            inst = p["call"]()
        if p["kind"] == "c":
            sem = SEM[q]
            inst.then_inc(T.sem[sem], 1)
            cnt[sem] = cnt.get(sem, 0) + 1
        elif p["kind"] == "d":
            sem = "d%d" % nd[0]
            nd[0] += 1
            inst.then_inc(T.sem[sem], 16)
            cnt[sem] = 16
        elif p["kind"] == "r":
            sem = "rl"
            cnt[sem] = cnt.get(sem, 0) + p["extra"][1]
        else:
            sem = p["extra"][0]
            cnt[sem] = p["extra"][1]
        ref[i] = (sem, cnt[sem])
        if p["kind"] != "n":
            snap[ref[i]] = dict(know[q])
    for sem in sorted(cnt):
        g.wait_ge(T.sem[sem], cnt[sem])
